import numpy as np
import ml_dtypes


def mxq(x, axis, fmt="e4m3"):
    dtype, down = {"e4m3": (ml_dtypes.float8_e4m3fn, 7), "e5m2": (ml_dtypes.float8_e5m2, 14)}[fmt]
    v = np.moveaxis(np.asarray(x, np.float32).astype(ml_dtypes.bfloat16).astype(np.float64), axis, -1)
    blocks = v.reshape(v.shape[:-1] + (-1, 32))
    amax = np.abs(blocks).max(-1, keepdims=True)
    byte = np.maximum(np.where(amax > 0, np.frexp(amax)[1] - 1 + 127, 0) - down, 1)
    scale = np.exp2(byte - 127.0)
    codes = (blocks / scale).astype(np.float32).astype(dtype).astype(np.float64)
    return np.moveaxis((codes * scale).reshape(v.shape), -1, axis)


WIDE = False


def mx_kscale(k):
    if not WIDE:
        return np.ones(k)
    levels = np.array([10, -10, 5, -5, 0])
    if k % 512:
        return np.exp2(np.random.permutation(np.resize(levels, k // 32))).repeat(32)
    a = np.empty((k // 512, 16))
    for p in range(k // 512):
        a[p, :8] = np.random.permutation(np.resize(levels, 8))
        for g in range(8):
            far = levels[np.abs(levels - a[p, g]) >= 10]
            a[p, g + 8] = far[np.random.randint(len(far))]
    return np.exp2(a.ravel()).repeat(32)


def f64(x):
    return np.asarray(x).astype(np.float64)


def striped(idx):
    return np.tile(idx.reshape(-1, 16).T, (8, 1)).astype(np.uint16)


def unstriped(offs):
    return offs[:16].T.reshape(-1).astype(np.int64)


def striped8(idx):
    return np.concatenate([x.reshape(-1, 16).T for x in idx]).astype(np.uint16)


def runs(offs, k):
    lists = np.stack([offs[16 * r : 16 * r + 16].T.reshape(-1) for r in range(8)]).astype(np.int64)
    return lists[np.arange(k) % 512 // 64]


def pack_weight(w):
    k, n = w.shape
    w = f64(np.asarray(w, np.float32).astype(ml_dtypes.bfloat16)).reshape(k // 32, 32, n)
    amax = np.abs(w).max(1)
    byte = np.clip(np.where(amax > 0, np.frexp(amax)[1] - 1 + 127 - 7, 1), 1, 254)
    scaled = (w * np.exp2(127.0 - byte)[:, None, :]).reshape(k, n).astype(np.float32)
    words = np.ascontiguousarray(scaled.reshape(k // 512, 128, 4, n).transpose(0, 1, 3, 2)).astype(ml_dtypes.float8_e4m3fn).view(np.uint8)
    return words, np.ascontiguousarray(byte.astype(np.uint8).reshape(k // 512, 16, n))


def unpack_weight(words, scales):
    g, p, n, _ = words.shape
    vals = np.ascontiguousarray(words).view(ml_dtypes.float8_e4m3fn).astype(np.float64) * np.repeat(np.exp2(scales.astype(np.float64) - 127.0), 8, axis=1)[..., None]
    return vals.transpose(0, 1, 3, 2).reshape(g * 512, n)


E2M1 = np.array([0.0, 0.5, 1.0, 1.5, 2.0, 3.0, 4.0, 6.0, -0.0, -0.5, -1.0, -1.5, -2.0, -3.0, -4.0, -6.0])


def pack_fp4(w):
    k, n = w.shape
    w = f64(np.asarray(w, np.float32).astype(ml_dtypes.bfloat16)).reshape(k // 32, 32, n)
    amax = np.abs(w).max(1)
    mant, ex = np.frexp(amax / 6.0)
    byte = np.clip(np.where(amax > 0, np.where(mant > 0.5, ex, ex - 1) + 127, 1), 1, 254)
    scaled = (w * np.exp2(127.0 - byte)[:, None, :]).reshape(k, n).astype(np.float32)
    c = np.ascontiguousarray(scaled.reshape(k // 512, 128, 4, n).transpose(0, 1, 3, 2)).astype(ml_dtypes.float4_e2m1fn).view(np.uint8) & 0xF
    words = (c[..., 0::2] | (c[..., 1::2] << 4)).reshape(k // 512, 128, 2 * n)
    return np.ascontiguousarray(words), np.ascontiguousarray(byte.astype(np.uint8).reshape(k // 512, 16, n))


def unpack_fp4(words, scales):
    g, _, n = scales.shape
    words = np.ascontiguousarray(words).reshape(g, 128, n, 2)
    nib = np.empty((g, 128, n, 4), np.uint8)
    nib[..., 0::2] = words & 0xF
    nib[..., 1::2] = words >> 4
    vals = E2M1[nib] * np.repeat(np.exp2(scales.astype(np.float64) - 127.0), 8, axis=1)[..., None]
    return vals.transpose(0, 1, 3, 2).reshape(g * 512, n)


def sigmoid(v):
    return 1.0 / (1.0 + np.exp(-np.maximum(v, -700.0)))

def planes(y):
    n, m = y.shape
    v = y.astype(np.float32).astype(ml_dtypes.bfloat16).astype(np.float64).reshape(n // 32, 32, m)
    top = np.abs(v).max(1)
    byte = np.clip(np.where(top > 0, np.frexp(top)[1] - 1 + 127 - 7, 1), 1, 254)
    codes = (v * np.exp2(127.0 - byte)[:, None, :]).reshape(n, m).astype(np.float32).astype(ml_dtypes.float8_e4m3fn).view(np.uint8)
    words = codes.reshape(n // 512, 128, 4, m).transpose(0, 1, 3, 2)
    return np.ascontiguousarray(words), np.ascontiguousarray(byte.astype(np.uint8).reshape(n // 512, 16, m))


K, T, S, N, G, H = 512, 2048, 512, 512, 2048, 512


def setup_inputs():
    n = np.random.standard_normal
    s = mx_kscale(K)[:, None]
    u = mx_kscale(H)
    packed_xT = pack_weight(n((K, T)) * s)
    packed_dT = pack_weight(n((K, G)) / s)
    packed_w1 = pack_fp4(n((H, N)) / np.sqrt(H) / u[:, None])
    return {
        "x_words": packed_xT[0],
        "x_scales": packed_xT[1],
        "d_words": packed_dT[0],
        "d_scales": packed_dT[1],
        "gn": (np.random.uniform(0.5, 1.5, (H, 1)) * u[:, None]).astype(np.float32),
        "w1_words": packed_w1[0],
        "w1_scales": packed_w1[1],
        "offs": striped(np.random.permutation(T)[:S]),
        "k1": striped8(np.random.randint(0, G, (8, H))),
        "k2": striped8(np.random.randint(0, G, (8, H))),
    }


def reference(x_words, x_scales, d_words, d_scales, gn, w1_words, w1_scales, offs, k1, k2):
    d_k1 = unpack_weight(d_words, d_scales)[np.arange(K)[:, None], runs(k1, K)]
    xq = unpack_weight(x_words, x_scales)[:, unstriped(offs)]
    a = 0.0625 * (d_k1.T @ xq)
    d_k2 = unpack_weight(d_words, d_scales)[np.arange(K)[:, None], runs(k2, K)]
    b = 0.0625 * (d_k2.T @ xq)
    z = f64(gn) * (a * sigmoid(b))
    out_0 = unpack_fp4(w1_words, w1_scales).T @ mxq(z, 0, "e4m3")
    return (out_0,) + planes(out_0)

@@ -1,0 +1,187 @@
+from contextlib import ExitStack
+
+import concourse.mybir as mybir
+
+K, T, S, N, G, H = 512, 2048, 512, 512, 2048, 512
+FLOPS = 2 * K * H * S * 2 + 2 * H * N * S
+
+F32 = mybir.dt.float32
+BF16 = mybir.dt.bfloat16
+I32 = mybir.dt.int32
+U32 = mybir.dt.uint32
+U16 = mybir.dt.uint16
+U8 = mybir.dt.uint8
+FP8X4 = mybir.dt.float8_e4m3fn_x4
+FP4X4 = mybir.dt.float4_e2m1fn_x4
+ACT = mybir.ActivationFunctionType
+ALU = mybir.AluOpType
+
+P = 128
+PACK = 4
+CH = 128
+NCH = S // CH
+SCORE_SCALE = 0.0625
+
+
+def tile_picked_scoregate_sigmoid_po_kernel(
+    tc, x_words, x_scales, d_words, d_scales, gn, w1_words, w1_scales, offs, k1, k2, out_0, out_1, out_2
+):
+    nc = tc.nc
+    with ExitStack() as ctx:
+        sb = ctx.enter_context(tc.tile_pool(name="sb", bufs=1))
+        reuse = ctx.enter_context(tc.tile_pool(name="reuse", bufs=1))
+        psum = ctx.enter_context(tc.psum_pool(name="psum", bufs=1))
+
+        def tile(name, shape, dtype, tag=None):
+            return sb.tile(shape, dtype, name=name, tag=tag or name, align_bytes=64)
+
+        def placed(name, shape, dtype, offset):
+            return reuse.tile(shape, dtype, name=name, align_bytes=64, offset=offset)
+
+        k1_list = sb.tile([P, H // 16], U16, name="k1_list")
+        offs_list = sb.tile([P, S // 16], U16, name="offs_list")
+        k2_list = sb.tile([P, H // 16], U16, name="k2_list")
+        d_byte_table = tile("d_byte_table", [P, G], U8)
+        x_byte_table = tile("x_byte_table", [P, T], U8)
+        d_word_table = tile("d_word_table", [P, G], I32)
+        x_word_table = placed("x_word_table", [P, T], I32, 0)
+        gain = tile("gain", [P, PACK], F32)
+        gain_scaled = tile("gain_scaled", [P, PACK], F32)
+        warm = tile("warm", [P, PACK], F32)
+
+        def load_scale_rows(queue, table, source):
+            rows = source[0].bitcast(I32)
+            queue.dma_start(table[:].bitcast(I32), rows.unsqueeze(1).to_broadcast([16, 8, rows.shape[1]]))
+
+        load_scale_rows(nc.scalar, d_byte_table, d_scales)
+        nc.scalar.dma_start(gain[:], gn.rearrange("(p t) o -> p (t o)", t=PACK))
+        nc.sync.dma_start(k1_list[:], k1)
+        nc.sync.dma_start(offs_list[:], offs)
+        load_scale_rows(nc.sync, x_byte_table, x_scales)
+        nc.sync.dma_start(k2_list[:], k2)
+        nc.sync.dma_start(d_word_table[:], d_words[0].rearrange("p c r -> p (c r)").bitcast(I32))
+        nc.sync.dma_start(x_word_table[:], x_words[0].rearrange("p c r -> p (c r)").bitcast(I32))
+        nc.scalar.activation(warm[:], gain[:], ACT.Sigmoid)
+        nc.scalar.activation(gain_scaled[:], gain[:], ACT.Copy, scale=SCORE_SCALE)
+
+        def gather_words(name, table, offsets, tag=None):
+            picked = tile(name, [P, S], U32, tag)
+            nc.vector.tensor_copy(picked[:], table[:].bitcast(U32).indirect(offsets[:]))
+            return picked
+
+        def deal(dst, src):
+            nc.vector.tensor_copy(dst.rearrange("p (t m) -> p m t", t=PACK), src.rearrange("p (m t) -> p m t", t=PACK))
+
+        def place_scale_rows(planes, queues):
+            rows = planes[:].bitcast(I32)
+            for r in range(1, PACK):
+                queues[r - 1].dma_start(rows[r:P:32, :], rows[8 * r : P : 32, :])
+
+        planes_a = tile("planes_a", [P, H + S], U8)
+        planes_b = tile("planes_b", [P, H], U8)
+        k1_bytes = tile("k1_bytes", [P, H], U8)
+        x_bytes = tile("x_bytes", [P, S], U8)
+        k2_bytes = placed("k2_bytes", [P, H], U8, 8192 + 256)
+        nc.vector.tensor_copy(k1_bytes[:], d_byte_table[:].indirect(k1_list[:]))
+        nc.vector.tensor_copy(x_bytes[:], x_byte_table[:].indirect(offs_list[:]))
+        deal(planes_a[:, 0:H], k1_bytes[:])
+        nc.vector.tensor_copy(planes_a[:, H : H + S].bitcast(I32), x_bytes[:].bitcast(I32))
+        place_scale_rows(planes_a, (nc.scalar, nc.scalar, nc.scalar))
+        nc.vector.tensor_copy(k2_bytes[:], d_byte_table[:].indirect(k2_list[:]))
+        k1_picked = gather_words("k1_picked", d_word_table, k1_list)
+        deal(planes_b[:], k2_bytes[:])
+        place_scale_rows(planes_b, (nc.scalar, nc.scalar, nc.scalar))
+        w_bytes = placed("w_bytes", [P, N], U8, 8192)
+        w_words = placed("w_words", [P, 2 * N], U8, 8192 + N)
+        nc.sync.dma_start(w_words[:].bitcast(I32), w1_words[0].bitcast(I32))
+        w_rows = w1_scales[0].bitcast(I32)
+        for q in range(4):
+            nc.sync.dma_start(w_bytes[32 * q : 32 * q + 32, :].bitcast(I32),
+                              w_rows[4 * q : 4 * q + 4, :].unsqueeze(0).to_broadcast([8, 4, N // 4]))
+        x_codes = gather_words("x_codes", x_word_table, offs_list)
+        k1_codes = tile("k1_codes", [P, H], U32)
+        deal(k1_codes[:].bitcast(I32), k1_picked[:].bitcast(I32))
+        x_plane = planes_a[:, H : H + S]
+
+        weighted = tile("weighted", [P, PACK, S], F32)
+        for t in range(PACK):
+            cols = slice(t * P, (t + 1) * P)
+            bank = psum.tile([P, S], F32, name="a_bank", tag="bank%d" % t)
+            nc.tensor.matmul_mx(out=bank[:], lhsT=k1_codes[:, cols].bitcast(FP8X4), lhsT_scale=planes_a[:, cols],
+                                rhs=x_codes[:].bitcast(FP8X4), rhs_scale=x_plane, start=True, stop=True)
+            nc.scalar.activation(weighted[:, t, :], bank[:], ACT.Copy, scale=gain_scaled[:, t : t + 1])
+
+        k2_picked = placed("k2_picked", [P, H], U32, 0)
+        nc.vector.tensor_copy(k2_picked[:], d_word_table[:].bitcast(U32).indirect(k2_list[:]))
+        w_plane = placed("w_plane", [P, N], U8, 4096)
+        deal(w_plane[:], w_bytes[:])
+        k2_codes = tile("k2_codes", [P, H], U32)
+        deal(k2_codes[:].bitcast(I32), k2_picked[:].bitcast(I32))
+        w_codes = placed("w_codes", [P, 2 * N], U8, 0)
+        nc.vector.tensor_copy(w_codes[:].rearrange("p (t m b) -> p m t b", t=PACK, b=2),
+                              w_words[:].rearrange("p (m t b) -> p m t b", t=PACK, b=2))
+
+        z_codes = tile("z_codes", [P, S], U32)
+        z_plane = tile("z_plane", [P, S], U8)
+        y_codes = tile("y_codes", [P, S], U32)
+        y_plane = tile("y_plane", [P, S], U8)
+        out_rows = out_0.rearrange("(p t) j -> p t j", t=PACK)
+        out_words = out_1[0].rearrange("p c r -> p (c r)").bitcast(I32)
+        gates, zs, ys, yr = {}, {}, {}, {}
+
+        def chunk(c):
+            return slice(c * CH, (c + 1) * CH)
+
+        def gate(c):
+            bank = psum.tile([P, PACK, CH], F32, name="b_bank", tag="bank%d" % (PACK + c))
+            for t in range(PACK):
+                cols = slice(t * P, (t + 1) * P)
+                nc.tensor.matmul_mx(out=bank[:, t, :], lhsT=k2_codes[:, cols].bitcast(FP8X4), lhsT_scale=planes_b[:, cols],
+                                    rhs=x_codes[:, chunk(c)].bitcast(FP8X4), rhs_scale=x_plane[:, chunk(c)], start=True, stop=True)
+            gates[c] = tile("gate%d" % c, [P, CH // 4, PACK, 4], F32)
+            nc.scalar.activation(gates[c][:], bank[:].rearrange("p t (c i) -> p c t i", i=4), ACT.Sigmoid, scale=SCORE_SCALE)
+
+        def form_z(c):
+            zs[c] = tile("z%d" % c, [P, CH, PACK], BF16)
+            nc.vector.tensor_tensor(zs[c][:].rearrange("p (c i) t -> p c t i", i=4),
+                                    weighted[:, :, chunk(c)].rearrange("p t (c i) -> p c t i", i=4), gates[c][:], ALU.mult)
+
+        def quantize_z(c):
+            nc.vector.quantize_mx(out=z_codes[:, chunk(c)].bitcast(FP8X4), scales=z_plane[:, chunk(c)],
+                                  in_=zs[c][:].rearrange("p j t -> p (j t)"))
+
+        def project(c):
+            bank = psum.tile([P, PACK, CH], F32, name="y_bank", tag="bank%d" % c)
+            for t in range(PACK):
+                nc.tensor.matmul_mx(out=bank[:, t, :], lhsT=w_codes[:, 2 * t * P : 2 * (t + 1) * P].bitcast(FP4X4),
+                                    lhsT_scale=w_plane[:, t * P : (t + 1) * P],
+                                    rhs=z_codes[:, chunk(c)].bitcast(FP8X4), rhs_scale=z_plane[:, chunk(c)], start=True, stop=True)
+            ys[c] = tile("y%d" % c, [P, PACK, CH], F32)
+            nc.scalar.copy(ys[c][:], bank[:])
+            nc.sync.dma_start(out_rows[:, :, chunk(c)], ys[c][:])
+
+        def round_y(c):
+            yr[c] = tile("yr%d" % c, [P, CH, PACK], BF16)
+            nc.vector.tensor_copy(yr[c][:].rearrange("p (c i) t -> p c t i", i=4), ys[c][:].rearrange("p t (c i) -> p c t i", i=4))
+
+        def quantize_y(c):
+            nc.vector.quantize_mx(out=y_codes[:, chunk(c)].bitcast(FP8X4), scales=y_plane[:, chunk(c)],
+                                  in_=yr[c][:].rearrange("p j t -> p (j t)"))
+            nc.sync.dma_start(out_words[:, chunk(c)], y_codes[:, chunk(c)].bitcast(I32))
+
+        for c in range(NCH):
+            gate(c)
+        for c in range(NCH + 1):
+            if c < NCH:
+                form_z(c)
+            if c >= 1:
+                quantize_z(c - 1)
+                project(c - 1)
+        for c in range(NCH + 1):
+            if c < NCH:
+                round_y(c)
+            if c >= 1:
+                quantize_y(c - 1)
+        for q in range(4):
+            queue = nc.scalar if q % 2 else nc.sync
+            queue.dma_start(out_2[0, 4 * q : 4 * q + 4, :].bitcast(I32), y_plane[32 * q : 32 * q + 4, :].bitcast(I32))

@@ -21,6 +21,7 @@ PACK = 4
 CH = 128
 NCH = S // CH
 SCORE_SCALE = 0.0625
+WARM_PASSES = 3
 
 
 def tile_picked_scoregate_sigmoid_po_kernel(
@@ -56,9 +57,9 @@ def tile_picked_scoregate_sigmoid_po_kernel(
         load_scale_rows(nc.scalar, d_byte_table, d_scales)
         nc.scalar.dma_start(gain[:], gn.rearrange("(p t) o -> p (t o)", t=PACK))
         nc.sync.dma_start(k1_list[:], k1)
+        nc.sync.dma_start(k2_list[:], k2)
         nc.sync.dma_start(offs_list[:], offs)
         load_scale_rows(nc.sync, x_byte_table, x_scales)
-        nc.sync.dma_start(k2_list[:], k2)
         nc.sync.dma_start(d_word_table[:], d_words[0].rearrange("p c r -> p (c r)").bitcast(I32))
         nc.sync.dma_start(x_word_table[:], x_words[0].rearrange("p c r -> p (c r)").bitcast(I32))
         nc.scalar.activation(warm[:], gain[:], ACT.Sigmoid)
@@ -77,20 +78,16 @@ def tile_picked_scoregate_sigmoid_po_kernel(
             for r in range(1, PACK):
                 queues[r - 1].dma_start(rows[r:P:32, :], rows[8 * r : P : 32, :])
 
-        planes_a = tile("planes_a", [P, H + S], U8)
-        planes_b = tile("planes_b", [P, H], U8)
-        k1_bytes = tile("k1_bytes", [P, H], U8)
-        x_bytes = tile("x_bytes", [P, S], U8)
-        k2_bytes = placed("k2_bytes", [P, H], U8, 8192 + 256)
-        nc.vector.tensor_copy(k1_bytes[:], d_byte_table[:].indirect(k1_list[:]))
+        planes = tile("planes", [P, 2 * H + S], U8)
+        key_bytes = tile("key_bytes", [P, 2, H], U8)
+        nc.vector.tensor_copy(key_bytes[:, 0, :], d_byte_table[:].indirect(k1_list[:]))
+        nc.vector.tensor_copy(key_bytes[:, 1, :], d_byte_table[:].indirect(k2_list[:]))
+        x_bytes = placed("x_bytes", [P, S], U8, 8192 + 256)
         nc.vector.tensor_copy(x_bytes[:], x_byte_table[:].indirect(offs_list[:]))
-        deal(planes_a[:, 0:H], k1_bytes[:])
-        nc.vector.tensor_copy(planes_a[:, H : H + S].bitcast(I32), x_bytes[:].bitcast(I32))
-        place_scale_rows(planes_a, (nc.scalar, nc.scalar, nc.scalar))
-        nc.vector.tensor_copy(k2_bytes[:], d_byte_table[:].indirect(k2_list[:]))
-        k1_picked = gather_words("k1_picked", d_word_table, k1_list)
-        deal(planes_b[:], k2_bytes[:])
-        place_scale_rows(planes_b, (nc.scalar, nc.scalar, nc.scalar))
+        nc.vector.tensor_copy(planes[:, 0 : 2 * H].rearrange("p (l t m) -> p l m t", l=2, t=PACK),
+                              key_bytes[:].rearrange("p l (m t) -> p l m t", t=PACK))
+        nc.vector.tensor_copy(planes[:, 2 * H : 2 * H + S].bitcast(I32), x_bytes[:].bitcast(I32))
+        place_scale_rows(planes, (nc.scalar, nc.scalar, nc.scalar))
         w_bytes = placed("w_bytes", [P, N], U8, 8192)
         w_words = placed("w_words", [P, 2 * N], U8, 8192 + N)
         nc.sync.dma_start(w_words[:].bitcast(I32), w1_words[0].bitcast(I32))
@@ -98,25 +95,34 @@ def tile_picked_scoregate_sigmoid_po_kernel(
         for q in range(4):
             nc.sync.dma_start(w_bytes[32 * q : 32 * q + 32, :].bitcast(I32),
                               w_rows[4 * q : 4 * q + 4, :].unsqueeze(0).to_broadcast([8, 4, N // 4]))
+        k1_picked = gather_words("k1_picked", d_word_table, k1_list)
+        for w in range(WARM_PASSES):
+            bank = psum.tile([P, S], F32, name="warm_bank", tag="bank%d" % (PACK + w))
+            nc.tensor.matmul_mx(out=bank[:], lhsT=k1_picked[:, 0:P].bitcast(FP8X4), lhsT_scale=key_bytes[:, 0, 0:P],
+                                rhs=k1_picked[:].bitcast(FP8X4), rhs_scale=key_bytes[:, 0, :], start=True, stop=True)
         x_codes = gather_words("x_codes", x_word_table, offs_list)
         k1_codes = tile("k1_codes", [P, H], U32)
         deal(k1_codes[:].bitcast(I32), k1_picked[:].bitcast(I32))
-        x_plane = planes_a[:, H : H + S]
+        x_plane = planes[:, 2 * H : 2 * H + S]
 
+        a_banks = []
         weighted = tile("weighted", [P, PACK, S], F32)
         for t in range(PACK):
             cols = slice(t * P, (t + 1) * P)
             bank = psum.tile([P, S], F32, name="a_bank", tag="bank%d" % t)
-            nc.tensor.matmul_mx(out=bank[:], lhsT=k1_codes[:, cols].bitcast(FP8X4), lhsT_scale=planes_a[:, cols],
+            nc.tensor.matmul_mx(out=bank[:], lhsT=k1_codes[:, cols].bitcast(FP8X4), lhsT_scale=planes[:, cols],
                                 rhs=x_codes[:].bitcast(FP8X4), rhs_scale=x_plane, start=True, stop=True)
-            nc.scalar.activation(weighted[:, t, :], bank[:], ACT.Copy, scale=gain_scaled[:, t : t + 1])
+            a_banks.append(bank)
+            if t < PACK - 1:
+                nc.scalar.activation(weighted[:, t, :], bank[:], ACT.Copy, scale=gain_scaled[:, t : t + 1])
 
         k2_picked = placed("k2_picked", [P, H], U32, 0)
         nc.vector.tensor_copy(k2_picked[:], d_word_table[:].bitcast(U32).indirect(k2_list[:]))
-        w_plane = placed("w_plane", [P, N], U8, 4096)
-        deal(w_plane[:], w_bytes[:])
         k2_codes = tile("k2_codes", [P, H], U32)
         deal(k2_codes[:].bitcast(I32), k2_picked[:].bitcast(I32))
+        nc.vector.tensor_scalar(weighted[:, PACK - 1, :], a_banks[PACK - 1][:], gain_scaled[:, PACK - 1 : PACK], None, ALU.mult)
+        w_plane = placed("w_plane", [P, N], U8, 1024)
+        deal(w_plane[:], w_bytes[:])
         w_codes = placed("w_codes", [P, 2 * N], U8, 0)
         nc.vector.tensor_copy(w_codes[:].rearrange("p (t m b) -> p m t b", t=PACK, b=2),
                               w_words[:].rearrange("p (m t b) -> p m t b", t=PACK, b=2))
@@ -136,7 +142,7 @@ def tile_picked_scoregate_sigmoid_po_kernel(
             bank = psum.tile([P, PACK, CH], F32, name="b_bank", tag="bank%d" % (PACK + c))
             for t in range(PACK):
                 cols = slice(t * P, (t + 1) * P)
-                nc.tensor.matmul_mx(out=bank[:, t, :], lhsT=k2_codes[:, cols].bitcast(FP8X4), lhsT_scale=planes_b[:, cols],
+                nc.tensor.matmul_mx(out=bank[:, t, :], lhsT=k2_codes[:, cols].bitcast(FP8X4), lhsT_scale=planes[:, H + t * P : H + (t + 1) * P],
                                     rhs=x_codes[:, chunk(c)].bitcast(FP8X4), rhs_scale=x_plane[:, chunk(c)], start=True, stop=True)
             gates[c] = tile("gate%d" % c, [P, CH // 4, PACK, 4], F32)
             nc.scalar.activation(gates[c][:], bank[:].rearrange("p t (c i) -> p c t i", i=4), ACT.Sigmoid, scale=SCORE_SCALE)

@@ -84,8 +84,8 @@ def tile_picked_scoregate_sigmoid_po_kernel(
         nc.vector.tensor_copy(key_bytes[:, 1, :], d_byte_table[:].indirect(k2_list[:]))
         x_bytes = placed("x_bytes", [P, S], U8, 8192 + 256)
         nc.vector.tensor_copy(x_bytes[:], x_byte_table[:].indirect(offs_list[:]))
-        nc.vector.tensor_copy(planes[:, 0 : 2 * H].rearrange("p (l t m) -> p l m t", l=2, t=PACK),
-                              key_bytes[:].rearrange("p l (m t) -> p l m t", t=PACK))
+        nc.vector.tensor_copy(planes[:, 0 : 2 * H].rearrange("p (l t m) -> p l t m", l=2, t=PACK),
+                              key_bytes[:].rearrange("p l (m t) -> p l t m", t=PACK))
         nc.vector.tensor_copy(planes[:, 2 * H : 2 * H + S].bitcast(I32), x_bytes[:].bitcast(I32))
         place_scale_rows(planes, (nc.scalar, nc.scalar, nc.scalar))
         w_bytes = placed("w_bytes", [P, N], U8, 8192)
@@ -118,14 +118,14 @@ def tile_picked_scoregate_sigmoid_po_kernel(
 
         k2_picked = placed("k2_picked", [P, H], U32, 0)
         nc.vector.tensor_copy(k2_picked[:], d_word_table[:].bitcast(U32).indirect(k2_list[:]))
+        w_plane = placed("w_plane", [P, N], U8, 4096)
+        nc.vector.tensor_copy(w_plane[:].rearrange("p (t m) -> p t m", t=PACK), w_bytes[:].rearrange("p (m t) -> p t m", t=PACK))
         k2_codes = tile("k2_codes", [P, H], U32)
         deal(k2_codes[:].bitcast(I32), k2_picked[:].bitcast(I32))
         nc.vector.tensor_scalar(weighted[:, PACK - 1, :], a_banks[PACK - 1][:], gain_scaled[:, PACK - 1 : PACK], None, ALU.mult)
-        w_plane = placed("w_plane", [P, N], U8, 1024)
-        deal(w_plane[:], w_bytes[:])
         w_codes = placed("w_codes", [P, 2 * N], U8, 0)
-        nc.vector.tensor_copy(w_codes[:].rearrange("p (t m b) -> p m t b", t=PACK, b=2),
-                              w_words[:].rearrange("p (m t b) -> p m t b", t=PACK, b=2))
+        nc.vector.tensor_copy(w_codes[:].rearrange("p (t m b) -> p t m b", t=PACK, b=2),
+                              w_words[:].rearrange("p (m t b) -> p t m b", t=PACK, b=2))
 
         z_codes = tile("z_codes", [P, S], U32)
         z_plane = tile("z_plane", [P, S], U8)
@@ -144,13 +144,13 @@ def tile_picked_scoregate_sigmoid_po_kernel(
                 cols = slice(t * P, (t + 1) * P)
                 nc.tensor.matmul_mx(out=bank[:, t, :], lhsT=k2_codes[:, cols].bitcast(FP8X4), lhsT_scale=planes[:, H + t * P : H + (t + 1) * P],
                                     rhs=x_codes[:, chunk(c)].bitcast(FP8X4), rhs_scale=x_plane[:, chunk(c)], start=True, stop=True)
-            gates[c] = tile("gate%d" % c, [P, CH // 4, PACK, 4], F32)
-            nc.scalar.activation(gates[c][:], bank[:].rearrange("p t (c i) -> p c t i", i=4), ACT.Sigmoid, scale=SCORE_SCALE)
+            gates[c] = tile("gate%d" % c, [P, CH // 2, PACK, 2], F32)
+            nc.scalar.activation(gates[c][:], bank[:].rearrange("p t (c i) -> p c t i", i=2), ACT.Sigmoid, scale=SCORE_SCALE)
 
         def form_z(c):
             zs[c] = tile("z%d" % c, [P, CH, PACK], BF16)
-            nc.vector.tensor_tensor(zs[c][:].rearrange("p (c i) t -> p c t i", i=4),
-                                    weighted[:, :, chunk(c)].rearrange("p t (c i) -> p c t i", i=4), gates[c][:], ALU.mult)
+            nc.vector.tensor_tensor(zs[c][:].rearrange("p (c i) t -> p c t i", i=2),
+                                    weighted[:, :, chunk(c)].rearrange("p t (c i) -> p c t i", i=2), gates[c][:], ALU.mult)
 
         def quantize_z(c):
             nc.vector.quantize_mx(out=z_codes[:, chunk(c)].bitcast(FP8X4), scales=z_plane[:, chunk(c)],
@@ -168,7 +168,7 @@ def tile_picked_scoregate_sigmoid_po_kernel(
 
         def round_y(c):
             yr[c] = tile("yr%d" % c, [P, CH, PACK], BF16)
-            nc.vector.tensor_copy(yr[c][:].rearrange("p (c i) t -> p c t i", i=4), ys[c][:].rearrange("p t (c i) -> p c t i", i=4))
+            nc.vector.tensor_copy(yr[c][:].rearrange("p (c i) t -> p c t i", i=2), ys[c][:].rearrange("p t (c i) -> p c t i", i=2))
 
         def quantize_y(c):
             nc.vector.quantize_mx(out=y_codes[:, chunk(c)].bitcast(FP8X4), scales=y_plane[:, chunk(c)],

@@ -22,6 +22,7 @@ CH = 128
 NCH = S // CH
 SCORE_SCALE = 0.0625
 WARM_PASSES = 3
+HALF = H // 2
 
 
 def tile_picked_scoregate_sigmoid_po_kernel(
@@ -65,13 +66,16 @@ def tile_picked_scoregate_sigmoid_po_kernel(
         nc.scalar.activation(warm[:], gain[:], ACT.Sigmoid)
         nc.scalar.activation(gain_scaled[:], gain[:], ACT.Copy, scale=SCORE_SCALE)
 
-        def gather_words(name, table, offsets, tag=None):
-            picked = tile(name, [P, S], U32, tag)
-            nc.vector.tensor_copy(picked[:], table[:].bitcast(U32).indirect(offsets[:]))
-            return picked
+        def gather_keys(picked, offsets):
+            for h in range(2):
+                nc.vector.tensor_copy(picked[:, h * HALF : (h + 1) * HALF],
+                                      d_word_table[:].bitcast(U32).indirect(offsets[:, h * HALF // 16 : (h + 1) * HALF // 16]))
 
-        def deal(dst, src):
-            nc.vector.tensor_copy(dst.rearrange("p (t m) -> p m t", t=PACK), src.rearrange("p (m t) -> p m t", t=PACK))
+        def deal_keys(codes, picked):
+            dst = codes[:].bitcast(I32).rearrange("p (t h m) -> p h m t", t=PACK, h=2)
+            src = picked[:].bitcast(I32).rearrange("p (h m t) -> p h m t", t=PACK, h=2)
+            for h in range(2):
+                nc.vector.tensor_copy(dst[:, h], src[:, h])
 
         def place_scale_rows(planes, queues):
             rows = planes[:].bitcast(I32)
@@ -95,14 +99,16 @@ def tile_picked_scoregate_sigmoid_po_kernel(
         for q in range(4):
             nc.sync.dma_start(w_bytes[32 * q : 32 * q + 32, :].bitcast(I32),
                               w_rows[4 * q : 4 * q + 4, :].unsqueeze(0).to_broadcast([8, 4, N // 4]))
-        k1_picked = gather_words("k1_picked", d_word_table, k1_list)
+        k1_picked = tile("k1_picked", [P, H], U32)
+        gather_keys(k1_picked, k1_list)
         for w in range(WARM_PASSES):
             bank = psum.tile([P, S], F32, name="warm_bank", tag="bank%d" % (PACK + w))
             nc.tensor.matmul_mx(out=bank[:], lhsT=k1_picked[:, 0:P].bitcast(FP8X4), lhsT_scale=key_bytes[:, 0, 0:P],
                                 rhs=k1_picked[:].bitcast(FP8X4), rhs_scale=key_bytes[:, 0, :], start=True, stop=True)
-        x_codes = gather_words("x_codes", x_word_table, offs_list)
         k1_codes = tile("k1_codes", [P, H], U32)
-        deal(k1_codes[:].bitcast(I32), k1_picked[:].bitcast(I32))
+        deal_keys(k1_codes, k1_picked)
+        x_codes = tile("x_codes", [P, S], U32)
+        nc.vector.tensor_copy(x_codes[:], x_word_table[:].bitcast(U32).indirect(offs_list[:]))
         x_plane = planes[:, 2 * H : 2 * H + S]
 
         a_banks = []
@@ -117,12 +123,12 @@ def tile_picked_scoregate_sigmoid_po_kernel(
                 nc.scalar.activation(weighted[:, t, :], bank[:], ACT.Copy, scale=gain_scaled[:, t : t + 1])
 
         k2_picked = placed("k2_picked", [P, H], U32, 0)
-        nc.vector.tensor_copy(k2_picked[:], d_word_table[:].bitcast(U32).indirect(k2_list[:]))
-        w_plane = placed("w_plane", [P, N], U8, 4096)
-        nc.vector.tensor_copy(w_plane[:].rearrange("p (t m) -> p t m", t=PACK), w_bytes[:].rearrange("p (m t) -> p t m", t=PACK))
+        gather_keys(k2_picked, k2_list)
         k2_codes = tile("k2_codes", [P, H], U32)
-        deal(k2_codes[:].bitcast(I32), k2_picked[:].bitcast(I32))
+        deal_keys(k2_codes, k2_picked)
         nc.vector.tensor_scalar(weighted[:, PACK - 1, :], a_banks[PACK - 1][:], gain_scaled[:, PACK - 1 : PACK], None, ALU.mult)
+        w_plane = placed("w_plane", [P, N], U8, 1024)
+        nc.vector.tensor_copy(w_plane[:].rearrange("p (t m) -> p t m", t=PACK), w_bytes[:].rearrange("p (m t) -> p t m", t=PACK))
         w_codes = placed("w_codes", [P, 2 * N], U8, 0)
         nc.vector.tensor_copy(w_codes[:].rearrange("p (t m b) -> p t m b", t=PACK, b=2),
                               w_words[:].rearrange("p (m t b) -> p t m b", t=PACK, b=2))
@@ -139,7 +145,7 @@ def tile_picked_scoregate_sigmoid_po_kernel(
             return slice(c * CH, (c + 1) * CH)
 
         def gate(c):
-            bank = psum.tile([P, PACK, CH], F32, name="b_bank", tag="bank%d" % (PACK + c))
+            bank = psum.tile([P, PACK, CH], F32, name="b_bank", tag="bank%d" % (PACK + c % 2))
             for t in range(PACK):
                 cols = slice(t * P, (t + 1) * P)
                 nc.tensor.matmul_mx(out=bank[:, t, :], lhsT=k2_codes[:, cols].bitcast(FP8X4), lhsT_scale=planes[:, H + t * P : H + (t + 1) * P],
@@ -173,7 +179,9 @@ def tile_picked_scoregate_sigmoid_po_kernel(
         def quantize_y(c):
             nc.vector.quantize_mx(out=y_codes[:, chunk(c)].bitcast(FP8X4), scales=y_plane[:, chunk(c)],
                                   in_=yr[c][:].rearrange("p j t -> p (j t)"))
-            nc.sync.dma_start(out_words[:, chunk(c)], y_codes[:, chunk(c)].bitcast(I32))
+            if c >= NCH - 2:
+                cols = chunk(c) if c == NCH - 1 else slice(0, (c + 1) * CH)
+                nc.sync.dma_start(out_words[:, cols], y_codes[:, cols].bitcast(I32))
 
         for c in range(NCH):
             gate(c)

@@ -21,7 +21,6 @@ PACK = 4
 CH = 128
 NCH = S // CH
 SCORE_SCALE = 0.0625
-WARM_PASSES = 3
 HALF = H // 2
 
 
@@ -34,11 +33,14 @@ def tile_picked_scoregate_sigmoid_po_kernel(
         reuse = ctx.enter_context(tc.tile_pool(name="reuse", bufs=1))
         psum = ctx.enter_context(tc.psum_pool(name="psum", bufs=1))
 
-        def tile(name, shape, dtype, tag=None):
-            return sb.tile(shape, dtype, name=name, tag=tag or name, align_bytes=64)
+        def tile(name, shape, dtype):
+            return sb.tile(shape, dtype, name=name, tag=name, align_bytes=64)
 
         def placed(name, shape, dtype, offset):
             return reuse.tile(shape, dtype, name=name, align_bytes=64, offset=offset)
+
+        def bank(name, shape, number):
+            return psum.tile(shape, F32, name=name, tag="bank%d" % number)
 
         k1_list = sb.tile([P, H // 16], U16, name="k1_list")
         offs_list = sb.tile([P, S // 16], U16, name="offs_list")
@@ -46,7 +48,7 @@ def tile_picked_scoregate_sigmoid_po_kernel(
         d_byte_table = tile("d_byte_table", [P, G], U8)
         x_byte_table = tile("x_byte_table", [P, T], U8)
         d_word_table = tile("d_word_table", [P, G], I32)
-        x_word_table = placed("x_word_table", [P, T], I32, 0)
+        x_word_table = placed("x_word_table", [P, T], I32, 16384)
         gain = tile("gain", [P, PACK], F32)
         gain_scaled = tile("gain_scaled", [P, PACK], F32)
         warm = tile("warm", [P, PACK], F32)
@@ -56,80 +58,89 @@ def tile_picked_scoregate_sigmoid_po_kernel(
             queue.dma_start(table[:].bitcast(I32), rows.unsqueeze(1).to_broadcast([16, 8, rows.shape[1]]))
 
         load_scale_rows(nc.scalar, d_byte_table, d_scales)
-        nc.scalar.dma_start(gain[:], gn.rearrange("(p t) o -> p (t o)", t=PACK))
-        nc.sync.dma_start(k1_list[:], k1)
         nc.sync.dma_start(k2_list[:], k2)
         nc.sync.dma_start(offs_list[:], offs)
         load_scale_rows(nc.sync, x_byte_table, x_scales)
         nc.sync.dma_start(d_word_table[:], d_words[0].rearrange("p c r -> p (c r)").bitcast(I32))
+        nc.scalar.dma_start(gain[:], gn.rearrange("(p t) o -> p (t o)", t=PACK))
         nc.sync.dma_start(x_word_table[:], x_words[0].rearrange("p c r -> p (c r)").bitcast(I32))
+        nc.sync.dma_start(k1_list[:], k1)
         nc.scalar.activation(warm[:], gain[:], ACT.Sigmoid)
         nc.scalar.activation(gain_scaled[:], gain[:], ACT.Copy, scale=SCORE_SCALE)
 
         def gather_keys(picked, offsets):
             for h in range(2):
-                nc.vector.tensor_copy(picked[:, h * HALF : (h + 1) * HALF],
-                                      d_word_table[:].bitcast(U32).indirect(offsets[:, h * HALF // 16 : (h + 1) * HALF // 16]))
+                nc.vector.tensor_copy(picked[h], d_word_table[:].bitcast(U32).indirect(offsets[:, h * HALF // 16 : (h + 1) * HALF // 16]))
 
         def deal_keys(codes, picked):
             dst = codes[:].bitcast(I32).rearrange("p (t h m) -> p h m t", t=PACK, h=2)
-            src = picked[:].bitcast(I32).rearrange("p (h m t) -> p h m t", t=PACK, h=2)
             for h in range(2):
-                nc.vector.tensor_copy(dst[:, h], src[:, h])
+                nc.vector.tensor_copy(dst[:, h], picked[h].bitcast(I32).rearrange("p (m t) -> p m t", t=PACK))
+
+        def deal_bytes(plane, source):
+            nc.vector.tensor_copy(plane.rearrange("p (t m) -> p t m", t=PACK), source.rearrange("p (m t) -> p t m", t=PACK))
 
         def place_scale_rows(planes, queues):
             rows = planes[:].bitcast(I32)
             for r in range(1, PACK):
                 queues[r - 1].dma_start(rows[r:P:32, :], rows[8 * r : P : 32, :])
 
-        planes = tile("planes", [P, 2 * H + S], U8)
-        key_bytes = tile("key_bytes", [P, 2, H], U8)
-        nc.vector.tensor_copy(key_bytes[:, 0, :], d_byte_table[:].indirect(k1_list[:]))
-        nc.vector.tensor_copy(key_bytes[:, 1, :], d_byte_table[:].indirect(k2_list[:]))
-        x_bytes = placed("x_bytes", [P, S], U8, 8192 + 256)
+        gate_planes = tile("gate_planes", [P, H + S], U8)
+        k2_bytes = tile("k2_bytes", [P, H], U8)
+        x_bytes = placed("x_bytes", [P, S], U8, 12288 + 256)
+        nc.vector.tensor_copy(k2_bytes[:], d_byte_table[:].indirect(k2_list[:]))
         nc.vector.tensor_copy(x_bytes[:], x_byte_table[:].indirect(offs_list[:]))
-        nc.vector.tensor_copy(planes[:, 0 : 2 * H].rearrange("p (l t m) -> p l t m", l=2, t=PACK),
-                              key_bytes[:].rearrange("p l (m t) -> p l t m", t=PACK))
-        nc.vector.tensor_copy(planes[:, 2 * H : 2 * H + S].bitcast(I32), x_bytes[:].bitcast(I32))
-        place_scale_rows(planes, (nc.scalar, nc.scalar, nc.scalar))
-        w_bytes = placed("w_bytes", [P, N], U8, 8192)
-        w_words = placed("w_words", [P, 2 * N], U8, 8192 + N)
+        deal_bytes(gate_planes[:, 0:H], k2_bytes[:])
+        nc.vector.tensor_copy(gate_planes[:, H : H + S].bitcast(I32), x_bytes[:].bitcast(I32))
+        place_scale_rows(gate_planes, (nc.scalar, nc.scalar, nc.scalar))
+        x_plane = gate_planes[:, H : H + S]
+        w_bytes = placed("w_bytes", [P, N], U8, 12288)
+        w_words = placed("w_words", [P, 2 * N], U8, 12288 + N)
         nc.sync.dma_start(w_words[:].bitcast(I32), w1_words[0].bitcast(I32))
         w_rows = w1_scales[0].bitcast(I32)
         for q in range(4):
             nc.sync.dma_start(w_bytes[32 * q : 32 * q + 32, :].bitcast(I32),
                               w_rows[4 * q : 4 * q + 4, :].unsqueeze(0).to_broadcast([8, 4, N // 4]))
-        k1_picked = tile("k1_picked", [P, H], U32)
-        gather_keys(k1_picked, k1_list)
-        for w in range(WARM_PASSES):
-            bank = psum.tile([P, S], F32, name="warm_bank", tag="bank%d" % (PACK + w))
-            nc.tensor.matmul_mx(out=bank[:], lhsT=k1_picked[:, 0:P].bitcast(FP8X4), lhsT_scale=key_bytes[:, 0, 0:P],
-                                rhs=k1_picked[:].bitcast(FP8X4), rhs_scale=key_bytes[:, 0, :], start=True, stop=True)
-        k1_codes = tile("k1_codes", [P, H], U32)
-        deal_keys(k1_codes, k1_picked)
-        x_codes = tile("x_codes", [P, S], U32)
-        nc.vector.tensor_copy(x_codes[:], x_word_table[:].bitcast(U32).indirect(offs_list[:]))
-        x_plane = planes[:, 2 * H : 2 * H + S]
-
-        a_banks = []
-        weighted = tile("weighted", [P, PACK, S], F32)
-        for t in range(PACK):
-            cols = slice(t * P, (t + 1) * P)
-            bank = psum.tile([P, S], F32, name="a_bank", tag="bank%d" % t)
-            nc.tensor.matmul_mx(out=bank[:], lhsT=k1_codes[:, cols].bitcast(FP8X4), lhsT_scale=planes[:, cols],
-                                rhs=x_codes[:].bitcast(FP8X4), rhs_scale=x_plane, start=True, stop=True)
-            a_banks.append(bank)
-            if t < PACK - 1:
-                nc.scalar.activation(weighted[:, t, :], bank[:], ACT.Copy, scale=gain_scaled[:, t : t + 1])
-
-        k2_picked = placed("k2_picked", [P, H], U32, 0)
+        k2_picked = [placed("k2_picked%d" % h, [P, HALF], U32, 1024 + 4 * HALF * h)[:] for h in range(2)]
         gather_keys(k2_picked, k2_list)
         k2_codes = tile("k2_codes", [P, H], U32)
         deal_keys(k2_codes, k2_picked)
-        nc.vector.tensor_scalar(weighted[:, PACK - 1, :], a_banks[PACK - 1][:], gain_scaled[:, PACK - 1 : PACK], None, ALU.mult)
-        w_plane = placed("w_plane", [P, N], U8, 1024)
-        nc.vector.tensor_copy(w_plane[:].rearrange("p (t m) -> p t m", t=PACK), w_bytes[:].rearrange("p (m t) -> p t m", t=PACK))
-        w_codes = placed("w_codes", [P, 2 * N], U8, 0)
+        k1_bytes = placed("k1_bytes", [P, H], U8, 8192)
+        late_planes = tile("late_planes", [P, H], U8)
+        x_codes = [tile("x_codes0", [P, HALF], U32)]
+
+        def gather_queries(h):
+            nc.vector.tensor_copy(x_codes[h][:],
+                                  x_word_table[:].bitcast(U32).indirect(offs_list[:, h * HALF // 16 : (h + 1) * HALF // 16]))
+
+        gather_queries(0)
+        nc.vector.tensor_copy(k1_bytes[:], d_byte_table[:].indirect(k1_list[:]))
+        deal_bytes(late_planes[:], k1_bytes[:])
+        place_scale_rows(late_planes, (nc.sync, nc.sync, nc.sync))
+        x_codes.append(placed("x_codes1", [P, HALF], U32, 8192))
+        gather_queries(1)
+
+        gate = [tile("gate%d" % h, [P, PACK, HALF], F32) for h in range(2)]
+        for h in range(2):
+            sig = [tile("sig%d%d" % (h, u), [P, 2, HALF], F32) for u in range(2)]
+            js = slice(h * HALF, (h + 1) * HALF)
+            for u in range(2):
+                b_bank = bank("b_bank", [P, 2, HALF], PACK + 2 * h + u)
+                for v in range(2):
+                    cols = slice((2 * u + v) * P, (2 * u + v + 1) * P)
+                    nc.tensor.matmul_mx(out=b_bank[:, v, :], lhsT=k2_codes[:, cols].bitcast(FP8X4), lhsT_scale=gate_planes[:, cols],
+                                        rhs=x_codes[h][:].bitcast(FP8X4), rhs_scale=x_plane[:, js], start=True, stop=True)
+                nc.scalar.activation(sig[u][:], b_bank[:], ACT.Sigmoid, scale=SCORE_SCALE)
+            for t in range(PACK):
+                nc.scalar.activation(gate[h][:, t, :], sig[t // 2][:, t % 2, :], ACT.Copy, scale=gain_scaled[:, t : t + 1])
+
+        k1_picked = [placed("k1_picked%d" % h, [P, HALF], U32, 4096 + 12288 * h)[:] for h in range(2)]
+        gather_keys(k1_picked, k1_list)
+        k1_codes = tile("k1_codes", [P, H], U32)
+        deal_keys(k1_codes, k1_picked)
+        w_plane = placed("w_plane", [P, N], U8, 16384 + 512)
+        w_codes = placed("w_codes", [P, 2 * N], U8, 16384 - 512)
+        deal_bytes(w_plane[:], w_bytes[:])
         nc.vector.tensor_copy(w_codes[:].rearrange("p (t m b) -> p t m b", t=PACK, b=2),
                               w_words[:].rearrange("p (m t b) -> p t m b", t=PACK, b=2))
 
@@ -139,37 +150,36 @@ def tile_picked_scoregate_sigmoid_po_kernel(
         y_plane = tile("y_plane", [P, S], U8)
         out_rows = out_0.rearrange("(p t) j -> p t j", t=PACK)
         out_words = out_1[0].rearrange("p c r -> p (c r)").bitcast(I32)
-        gates, zs, ys, yr = {}, {}, {}, {}
+        scores, zs, ys, yr = {}, {}, {}, {}
 
         def chunk(c):
             return slice(c * CH, (c + 1) * CH)
 
-        def gate(c):
-            bank = psum.tile([P, PACK, CH], F32, name="b_bank", tag="bank%d" % (PACK + c % 2))
+        def score(c):
+            scores[c] = bank("a_bank", [P, PACK, CH], c)
             for t in range(PACK):
                 cols = slice(t * P, (t + 1) * P)
-                nc.tensor.matmul_mx(out=bank[:, t, :], lhsT=k2_codes[:, cols].bitcast(FP8X4), lhsT_scale=planes[:, H + t * P : H + (t + 1) * P],
-                                    rhs=x_codes[:, chunk(c)].bitcast(FP8X4), rhs_scale=x_plane[:, chunk(c)], start=True, stop=True)
-            gates[c] = tile("gate%d" % c, [P, CH // 2, PACK, 2], F32)
-            nc.scalar.activation(gates[c][:], bank[:].rearrange("p t (c i) -> p c t i", i=2), ACT.Sigmoid, scale=SCORE_SCALE)
+                nc.tensor.matmul_mx(out=scores[c][:, t, :], lhsT=k1_codes[:, cols].bitcast(FP8X4), lhsT_scale=late_planes[:, cols],
+                                    rhs=x_codes[c // 2][:, chunk(c % 2)].bitcast(FP8X4), rhs_scale=x_plane[:, chunk(c)], start=True, stop=True)
 
         def form_z(c):
             zs[c] = tile("z%d" % c, [P, CH, PACK], BF16)
             nc.vector.tensor_tensor(zs[c][:].rearrange("p (c i) t -> p c t i", i=2),
-                                    weighted[:, :, chunk(c)].rearrange("p t (c i) -> p c t i", i=2), gates[c][:], ALU.mult)
+                                    scores[c][:].rearrange("p t (c i) -> p c t i", i=2),
+                                    gate[c // 2][:, :, chunk(c % 2)].rearrange("p t (c i) -> p c t i", i=2), ALU.mult)
 
         def quantize_z(c):
             nc.vector.quantize_mx(out=z_codes[:, chunk(c)].bitcast(FP8X4), scales=z_plane[:, chunk(c)],
                                   in_=zs[c][:].rearrange("p j t -> p (j t)"))
 
         def project(c):
-            bank = psum.tile([P, PACK, CH], F32, name="y_bank", tag="bank%d" % c)
+            y_bank = bank("y_bank", [P, PACK, CH], PACK + c)
             for t in range(PACK):
-                nc.tensor.matmul_mx(out=bank[:, t, :], lhsT=w_codes[:, 2 * t * P : 2 * (t + 1) * P].bitcast(FP4X4),
+                nc.tensor.matmul_mx(out=y_bank[:, t, :], lhsT=w_codes[:, 2 * t * P : 2 * (t + 1) * P].bitcast(FP4X4),
                                     lhsT_scale=w_plane[:, t * P : (t + 1) * P],
                                     rhs=z_codes[:, chunk(c)].bitcast(FP8X4), rhs_scale=z_plane[:, chunk(c)], start=True, stop=True)
             ys[c] = tile("y%d" % c, [P, PACK, CH], F32)
-            nc.scalar.copy(ys[c][:], bank[:])
+            nc.scalar.copy(ys[c][:], y_bank[:])
             nc.sync.dma_start(out_rows[:, :, chunk(c)], ys[c][:])
 
         def round_y(c):
@@ -184,7 +194,7 @@ def tile_picked_scoregate_sigmoid_po_kernel(
                 nc.sync.dma_start(out_words[:, cols], y_codes[:, cols].bitcast(I32))
 
         for c in range(NCH):
-            gate(c)
+            score(c)
         for c in range(NCH + 1):
             if c < NCH:
                 form_z(c)

@@ -22,6 +22,7 @@ CH = 128
 NCH = S // CH
 SCORE_SCALE = 0.0625
 HALF = H // 2
+WARM_PASSES = 3
 
 
 def tile_picked_scoregate_sigmoid_po_kernel(
@@ -57,7 +58,7 @@ def tile_picked_scoregate_sigmoid_po_kernel(
             rows = source[0].bitcast(I32)
             queue.dma_start(table[:].bitcast(I32), rows.unsqueeze(1).to_broadcast([16, 8, rows.shape[1]]))
 
-        load_scale_rows(nc.scalar, d_byte_table, d_scales)
+        load_scale_rows(nc.sync, d_byte_table, d_scales)
         nc.sync.dma_start(k2_list[:], k2)
         nc.sync.dma_start(offs_list[:], offs)
         load_scale_rows(nc.sync, x_byte_table, x_scales)
@@ -87,24 +88,24 @@ def tile_picked_scoregate_sigmoid_po_kernel(
 
         gate_planes = tile("gate_planes", [P, H + S], U8)
         k2_bytes = tile("k2_bytes", [P, H], U8)
-        x_bytes = placed("x_bytes", [P, S], U8, 12288 + 256)
+        x_bytes = tile("x_bytes", [P, S], U8)
         nc.vector.tensor_copy(k2_bytes[:], d_byte_table[:].indirect(k2_list[:]))
         nc.vector.tensor_copy(x_bytes[:], x_byte_table[:].indirect(offs_list[:]))
         deal_bytes(gate_planes[:, 0:H], k2_bytes[:])
         nc.vector.tensor_copy(gate_planes[:, H : H + S].bitcast(I32), x_bytes[:].bitcast(I32))
         place_scale_rows(gate_planes, (nc.scalar, nc.scalar, nc.scalar))
         x_plane = gate_planes[:, H : H + S]
-        w_bytes = placed("w_bytes", [P, N], U8, 12288)
-        w_words = placed("w_words", [P, 2 * N], U8, 12288 + N)
+        k2_picked = [placed("k2_picked%d" % h, [P, HALF], U32, 1024 + 4 * HALF * h)[:] for h in range(2)]
+        gather_keys(k2_picked, k2_list)
+        k2_codes = tile("k2_codes", [P, H], U32)
+        deal_keys(k2_codes, k2_picked)
+        w_bytes = placed("w_bytes", [P, N], U8, 1024 + 512)
+        w_words = placed("w_words", [P, 2 * N], U8, 1024 + 1024)
         nc.sync.dma_start(w_words[:].bitcast(I32), w1_words[0].bitcast(I32))
         w_rows = w1_scales[0].bitcast(I32)
         for q in range(4):
             nc.sync.dma_start(w_bytes[32 * q : 32 * q + 32, :].bitcast(I32),
                               w_rows[4 * q : 4 * q + 4, :].unsqueeze(0).to_broadcast([8, 4, N // 4]))
-        k2_picked = [placed("k2_picked%d" % h, [P, HALF], U32, 1024 + 4 * HALF * h)[:] for h in range(2)]
-        gather_keys(k2_picked, k2_list)
-        k2_codes = tile("k2_codes", [P, H], U32)
-        deal_keys(k2_codes, k2_picked)
         k1_bytes = placed("k1_bytes", [P, H], U8, 8192)
         late_planes = tile("late_planes", [P, H], U8)
         x_codes = [tile("x_codes0", [P, HALF], U32)]
@@ -136,6 +137,11 @@ def tile_picked_scoregate_sigmoid_po_kernel(
 
         k1_picked = [placed("k1_picked%d" % h, [P, HALF], U32, 4096 + 12288 * h)[:] for h in range(2)]
         gather_keys(k1_picked, k1_list)
+        for w in range(WARM_PASSES):
+            warm_bank = bank("warm_bank", [P, S], 1 + w)
+            keys = k1_picked[0] if w < WARM_PASSES - 1 else x_codes[1][:]
+            nc.tensor.matmul_mx(out=warm_bank[:], lhsT=keys[:, 0:P].bitcast(FP8X4), lhsT_scale=x_plane[:, 0:P],
+                                rhs=k2_codes[:].bitcast(FP8X4), rhs_scale=gate_planes[:, 0:H], start=True, stop=True)
         k1_codes = tile("k1_codes", [P, H], U32)
         deal_keys(k1_codes, k1_picked)
         w_plane = placed("w_plane", [P, N], U8, 16384 + 512)

@@ -46,10 +46,10 @@ def tile_picked_scoregate_sigmoid_po_kernel(
         k1_list = sb.tile([P, H // 16], U16, name="k1_list")
         offs_list = sb.tile([P, S // 16], U16, name="offs_list")
         k2_list = sb.tile([P, H // 16], U16, name="k2_list")
-        d_byte_table = tile("d_byte_table", [P, G], U8)
+        d_byte_table = placed("d_byte_table", [P, G], U8, 8192)
         x_byte_table = tile("x_byte_table", [P, T], U8)
         d_word_table = tile("d_word_table", [P, G], I32)
-        x_word_table = placed("x_word_table", [P, T], I32, 16384)
+        x_word_table = tile("x_word_table", [P, T], I32)
         gain = tile("gain", [P, PACK], F32)
         gain_scaled = tile("gain_scaled", [P, PACK], F32)
         warm = tile("warm", [P, PACK], F32)
@@ -58,7 +58,7 @@ def tile_picked_scoregate_sigmoid_po_kernel(
             rows = source[0].bitcast(I32)
             queue.dma_start(table[:].bitcast(I32), rows.unsqueeze(1).to_broadcast([16, 8, rows.shape[1]]))
 
-        load_scale_rows(nc.sync, d_byte_table, d_scales)
+        load_scale_rows(nc.scalar, d_byte_table, d_scales)
         nc.sync.dma_start(k2_list[:], k2)
         nc.sync.dma_start(offs_list[:], offs)
         load_scale_rows(nc.sync, x_byte_table, x_scales)
@@ -88,25 +88,25 @@ def tile_picked_scoregate_sigmoid_po_kernel(
 
         gate_planes = tile("gate_planes", [P, H + S], U8)
         k2_bytes = tile("k2_bytes", [P, H], U8)
-        x_bytes = tile("x_bytes", [P, S], U8)
+        x_bytes = placed("x_bytes", [P, S], U8, 12288 + 256)
         nc.vector.tensor_copy(k2_bytes[:], d_byte_table[:].indirect(k2_list[:]))
         nc.vector.tensor_copy(x_bytes[:], x_byte_table[:].indirect(offs_list[:]))
         deal_bytes(gate_planes[:, 0:H], k2_bytes[:])
         nc.vector.tensor_copy(gate_planes[:, H : H + S].bitcast(I32), x_bytes[:].bitcast(I32))
         place_scale_rows(gate_planes, (nc.scalar, nc.scalar, nc.scalar))
         x_plane = gate_planes[:, H : H + S]
-        k2_picked = [placed("k2_picked%d" % h, [P, HALF], U32, 1024 + 4 * HALF * h)[:] for h in range(2)]
-        gather_keys(k2_picked, k2_list)
-        k2_codes = tile("k2_codes", [P, H], U32)
-        deal_keys(k2_codes, k2_picked)
-        w_bytes = placed("w_bytes", [P, N], U8, 1024 + 512)
-        w_words = placed("w_words", [P, 2 * N], U8, 1024 + 1024)
+        w_bytes = placed("w_bytes", [P, N], U8, 12288)
+        w_words = placed("w_words", [P, 2 * N], U8, 12288 + N)
         nc.sync.dma_start(w_words[:].bitcast(I32), w1_words[0].bitcast(I32))
         w_rows = w1_scales[0].bitcast(I32)
         for q in range(4):
             nc.sync.dma_start(w_bytes[32 * q : 32 * q + 32, :].bitcast(I32),
                               w_rows[4 * q : 4 * q + 4, :].unsqueeze(0).to_broadcast([8, 4, N // 4]))
-        k1_bytes = placed("k1_bytes", [P, H], U8, 8192)
+        k2_picked = [tile("k2_picked%d" % h, [P, HALF], U32)[:] for h in range(2)]
+        gather_keys(k2_picked, k2_list)
+        k2_codes = tile("k2_codes", [P, H], U32)
+        deal_keys(k2_codes, k2_picked)
+        k1_bytes = tile("k1_bytes", [P, H], U8)
         late_planes = tile("late_planes", [P, H], U8)
         x_codes = [tile("x_codes0", [P, HALF], U32)]
 
@@ -118,7 +118,7 @@ def tile_picked_scoregate_sigmoid_po_kernel(
         nc.vector.tensor_copy(k1_bytes[:], d_byte_table[:].indirect(k1_list[:]))
         deal_bytes(late_planes[:], k1_bytes[:])
         place_scale_rows(late_planes, (nc.sync, nc.sync, nc.sync))
-        x_codes.append(placed("x_codes1", [P, HALF], U32, 8192))
+        x_codes.append(placed("x_codes1", [P, HALF], U32, 8192 + 512))
         gather_queries(1)
 
         gate = [tile("gate%d" % h, [P, PACK, HALF], F32) for h in range(2)]
@@ -135,17 +135,16 @@ def tile_picked_scoregate_sigmoid_po_kernel(
             for t in range(PACK):
                 nc.scalar.activation(gate[h][:, t, :], sig[t // 2][:, t % 2, :], ACT.Copy, scale=gain_scaled[:, t : t + 1])
 
-        k1_picked = [placed("k1_picked%d" % h, [P, HALF], U32, 4096 + 12288 * h)[:] for h in range(2)]
+        k1_picked = [placed("k1_picked%d" % h, [P, HALF], U32, 8192 - 512 + 2048 * h)[:] for h in range(2)]
         gather_keys(k1_picked, k1_list)
         for w in range(WARM_PASSES):
             warm_bank = bank("warm_bank", [P, S], 1 + w)
-            keys = k1_picked[0] if w < WARM_PASSES - 1 else x_codes[1][:]
-            nc.tensor.matmul_mx(out=warm_bank[:], lhsT=keys[:, 0:P].bitcast(FP8X4), lhsT_scale=x_plane[:, 0:P],
+            nc.tensor.matmul_mx(out=warm_bank[:], lhsT=x_codes[min(w, 1)][:, 0:P].bitcast(FP8X4), lhsT_scale=k1_bytes[:, 0:P],
                                 rhs=k2_codes[:].bitcast(FP8X4), rhs_scale=gate_planes[:, 0:H], start=True, stop=True)
         k1_codes = tile("k1_codes", [P, H], U32)
         deal_keys(k1_codes, k1_picked)
-        w_plane = placed("w_plane", [P, N], U8, 16384 + 512)
-        w_codes = placed("w_codes", [P, 2 * N], U8, 16384 - 512)
+        w_plane = placed("w_plane", [P, N], U8, 8192)
+        w_codes = placed("w_codes", [P, 2 * N], U8, 8192 - 1024)
         deal_bytes(w_plane[:], w_bytes[:])
         nc.vector.tensor_copy(w_codes[:].rearrange("p (t m b) -> p t m b", t=PACK, b=2),
                               w_words[:].rearrange("p (m t b) -> p t m b", t=PACK, b=2))
@@ -169,7 +168,7 @@ def tile_picked_scoregate_sigmoid_po_kernel(
                                     rhs=x_codes[c // 2][:, chunk(c % 2)].bitcast(FP8X4), rhs_scale=x_plane[:, chunk(c)], start=True, stop=True)
 
         def form_z(c):
-            zs[c] = tile("z%d" % c, [P, CH, PACK], BF16)
+            zs[c] = placed("z%d" % c, [P, CH, PACK], BF16, 16384 + 1024 * c)
             nc.vector.tensor_tensor(zs[c][:].rearrange("p (c i) t -> p c t i", i=2),
                                     scores[c][:].rearrange("p t (c i) -> p c t i", i=2),
                                     gate[c // 2][:, :, chunk(c % 2)].rearrange("p t (c i) -> p c t i", i=2), ALU.mult)
@@ -187,9 +186,12 @@ def tile_picked_scoregate_sigmoid_po_kernel(
             ys[c] = tile("y%d" % c, [P, PACK, CH], F32)
             nc.scalar.copy(ys[c][:], y_bank[:])
             nc.sync.dma_start(out_rows[:, :, chunk(c)], ys[c][:])
+            if c == NCH - 1:
+                yr[c] = tile("yr%d" % c, [P, CH, PACK], BF16)
+                nc.scalar.copy(yr[c][:], y_bank[:].rearrange("p t j -> p j t"))
 
         def round_y(c):
-            yr[c] = tile("yr%d" % c, [P, CH, PACK], BF16)
+            yr[c] = placed("yr%d" % c, [P, CH, PACK], BF16, 16384 + 1024 * (NCH - 2 - c))
             nc.vector.tensor_copy(yr[c][:].rearrange("p (c i) t -> p c t i", i=2), ys[c][:].rearrange("p t (c i) -> p c t i", i=2))
 
         def quantize_y(c):
@@ -208,7 +210,7 @@ def tile_picked_scoregate_sigmoid_po_kernel(
                 quantize_z(c - 1)
                 project(c - 1)
         for c in range(NCH + 1):
-            if c < NCH:
+            if c < NCH - 1:
                 round_y(c)
             if c >= 1:
                 quantize_y(c - 1)

@@ -22,7 +22,6 @@ CH = 128
 NCH = S // CH
 SCORE_SCALE = 0.0625
 HALF = H // 2
-WARM_PASSES = 3
 
 
 def tile_picked_scoregate_sigmoid_po_kernel(
@@ -137,10 +136,6 @@ def tile_picked_scoregate_sigmoid_po_kernel(
 
         k1_picked = [placed("k1_picked%d" % h, [P, HALF], U32, 8192 - 512 + 2048 * h)[:] for h in range(2)]
         gather_keys(k1_picked, k1_list)
-        for w in range(WARM_PASSES):
-            warm_bank = bank("warm_bank", [P, S], 1 + w)
-            nc.tensor.matmul_mx(out=warm_bank[:], lhsT=x_codes[min(w, 1)][:, 0:P].bitcast(FP8X4), lhsT_scale=k1_bytes[:, 0:P],
-                                rhs=k2_codes[:].bitcast(FP8X4), rhs_scale=gate_planes[:, 0:H], start=True, stop=True)
         k1_codes = tile("k1_codes", [P, H], U32)
         deal_keys(k1_codes, k1_picked)
         w_plane = placed("w_plane", [P, N], U8, 8192)

@@ -53,20 +53,20 @@ def tile_picked_scoregate_sigmoid_po_kernel(
         gain_scaled = tile("gain_scaled", [P, PACK], F32)
         warm = tile("warm", [P, PACK], F32)
 
-        def load_scale_rows(queue, table, source):
-            rows = source[0].bitcast(I32)
-            queue.dma_start(table[:].bitcast(I32), rows.unsqueeze(1).to_broadcast([16, 8, rows.shape[1]]))
-
-        load_scale_rows(nc.scalar, d_byte_table, d_scales)
-        nc.sync.dma_start(k2_list[:], k2)
         nc.sync.dma_start(offs_list[:], offs)
-        load_scale_rows(nc.sync, x_byte_table, x_scales)
-        nc.sync.dma_start(d_word_table[:], d_words[0].rearrange("p c r -> p (c r)").bitcast(I32))
-        nc.scalar.dma_start(gain[:], gn.rearrange("(p t) o -> p (t o)", t=PACK))
-        nc.sync.dma_start(x_word_table[:], x_words[0].rearrange("p c r -> p (c r)").bitcast(I32))
+        nc.vector.memset(d_byte_table[:].bitcast(I32), 0)
+        nc.scalar.dma_start(x_byte_table[0:32, :].bitcast(I32), x_scales[0].bitcast(I32).unsqueeze(1).to_broadcast([16, 2, T // 4]))
+        for first, last in ((32, 64), (64, P)):
+            nc.vector.memset(x_byte_table[first:last, :].bitcast(I32), 0)
+        nc.sync.dma_start(k2_list[:], k2)
         nc.sync.dma_start(k1_list[:], k1)
-        nc.scalar.activation(warm[:], gain[:], ACT.Sigmoid)
-        nc.scalar.activation(gain_scaled[:], gain[:], ACT.Copy, scale=SCORE_SCALE)
+        nc.sync.dma_start(gain[:], gn.rearrange("(p t) o -> p (t o)", t=PACK))
+        nc.sync.dma_start(d_byte_table[0:P:8, :].bitcast(I32), d_scales[0].bitcast(I32))
+        nc.sync.dma_start(d_word_table[:], d_words[0].rearrange("p c r -> p (c r)").bitcast(I32))
+        nc.sync.dma_start(x_word_table[:], x_words[0].rearrange("p c r -> p (c r)").bitcast(I32))
+        nc.gpsimd.memset(warm[:, 0:1], 0.0)
+        nc.scalar.activation(warm[:, 1:2], warm[:, 0:1], ACT.Sigmoid)
+        nc.gpsimd.tensor_scalar_mul(gain_scaled[:], gain[:], SCORE_SCALE)
 
         def gather_keys(picked, offsets):
             for h in range(2):
@@ -85,15 +85,27 @@ def tile_picked_scoregate_sigmoid_po_kernel(
             for r in range(1, PACK):
                 queues[r - 1].dma_start(rows[r:P:32, :], rows[8 * r : P : 32, :])
 
-        gate_planes = tile("gate_planes", [P, H + S], U8)
+        gate_planes = tile("gate_planes", [P, H], U8)
+        x_plane = tile("x_plane", [P, S], U8)
+        nc.vector.memset(x_plane[:].bitcast(I32), 0)
         k2_bytes = tile("k2_bytes", [P, H], U8)
-        x_bytes = placed("x_bytes", [P, S], U8, 12288 + 256)
-        nc.vector.tensor_copy(k2_bytes[:], d_byte_table[:].indirect(k2_list[:]))
+        x_bytes = placed("x_bytes", [P, S], U8, 28672 - HALF)
         nc.vector.tensor_copy(x_bytes[:], x_byte_table[:].indirect(offs_list[:]))
+        nc.vector.tensor_copy(k2_bytes[:], d_byte_table[:].indirect(k2_list[:]))
+        for q in range(4):
+            nc.sync.dma_start(x_plane[32 * q : 32 * q + 4, :].bitcast(I32), x_bytes[8 * q : 8 * q + 8 : 2, :].bitcast(I32))
+        k1_bytes = [tile("k1_bytes0", [P, HALF], U8), placed("k1_bytes1", [P, HALF], U8, 28672)]
+
+        def gather_late_bytes(h):
+            nc.vector.tensor_copy(k1_bytes[h][:], d_byte_table[:].indirect(k1_list[:, h * HALF // 16 : (h + 1) * HALF // 16]))
+
+        gather_late_bytes(0)
         deal_bytes(gate_planes[:, 0:H], k2_bytes[:])
-        nc.vector.tensor_copy(gate_planes[:, H : H + S].bitcast(I32), x_bytes[:].bitcast(I32))
         place_scale_rows(gate_planes, (nc.scalar, nc.scalar, nc.scalar))
-        x_plane = gate_planes[:, H : H + S]
+        k2_picked = [placed("k2_picked%d" % h, [P, HALF], U32, 12288 + 2048 * h)[:] for h in range(2)]
+        gather_keys(k2_picked, k2_list)
+        k2_codes = tile("k2_codes", [P, H], U32)
+        deal_keys(k2_codes, k2_picked)
         w_bytes = placed("w_bytes", [P, N], U8, 12288)
         w_words = placed("w_words", [P, 2 * N], U8, 12288 + N)
         nc.sync.dma_start(w_words[:].bitcast(I32), w1_words[0].bitcast(I32))
@@ -101,12 +113,7 @@ def tile_picked_scoregate_sigmoid_po_kernel(
         for q in range(4):
             nc.sync.dma_start(w_bytes[32 * q : 32 * q + 32, :].bitcast(I32),
                               w_rows[4 * q : 4 * q + 4, :].unsqueeze(0).to_broadcast([8, 4, N // 4]))
-        k2_picked = [tile("k2_picked%d" % h, [P, HALF], U32)[:] for h in range(2)]
-        gather_keys(k2_picked, k2_list)
-        k2_codes = tile("k2_codes", [P, H], U32)
-        deal_keys(k2_codes, k2_picked)
-        k1_bytes = tile("k1_bytes", [P, H], U8)
-        late_planes = tile("late_planes", [P, H], U8)
+        late_planes = placed("late_planes", [P, H], U8, 28672 - H)
         x_codes = [tile("x_codes0", [P, HALF], U32)]
 
         def gather_queries(h):
@@ -114,13 +121,16 @@ def tile_picked_scoregate_sigmoid_po_kernel(
                                   x_word_table[:].bitcast(U32).indirect(offs_list[:, h * HALF // 16 : (h + 1) * HALF // 16]))
 
         gather_queries(0)
-        nc.vector.tensor_copy(k1_bytes[:], d_byte_table[:].indirect(k1_list[:]))
-        deal_bytes(late_planes[:], k1_bytes[:])
+        gather_late_bytes(1)
+        late_slots = late_planes[:].rearrange("p (t h m) -> p h t m", t=PACK, h=2)
+        for h in range(2):
+            nc.vector.tensor_copy(late_slots[:, h], k1_bytes[h][:].rearrange("p (m t) -> p t m", t=PACK))
         place_scale_rows(late_planes, (nc.sync, nc.sync, nc.sync))
         x_codes.append(placed("x_codes1", [P, HALF], U32, 8192 + 512))
         gather_queries(1)
 
-        gate = [tile("gate%d" % h, [P, PACK, HALF], F32) for h in range(2)]
+        first_gate = tile("first_gate", [P, PACK, HALF], F32)
+        gate = [first_gate[:, :, 0:CH], first_gate[:, :, CH:HALF]] + [tile("gate%d" % c, [P, PACK, CH], F32)[:] for c in (2, 3)]
         for h in range(2):
             sig = [tile("sig%d%d" % (h, u), [P, 2, HALF], F32) for u in range(2)]
             js = slice(h * HALF, (h + 1) * HALF)
@@ -131,8 +141,10 @@ def tile_picked_scoregate_sigmoid_po_kernel(
                     nc.tensor.matmul_mx(out=b_bank[:, v, :], lhsT=k2_codes[:, cols].bitcast(FP8X4), lhsT_scale=gate_planes[:, cols],
                                         rhs=x_codes[h][:].bitcast(FP8X4), rhs_scale=x_plane[:, js], start=True, stop=True)
                 nc.scalar.activation(sig[u][:], b_bank[:], ACT.Sigmoid, scale=SCORE_SCALE)
-            for t in range(PACK):
-                nc.scalar.activation(gate[h][:, t, :], sig[t // 2][:, t % 2, :], ACT.Copy, scale=gain_scaled[:, t : t + 1])
+            pieces = [(first_gate[:], 0, HALF)] if h == 0 else [(gate[2], 0, CH), (gate[3], CH, HALF)]
+            for weighted, first, last in pieces:
+                for t in range(PACK):
+                    nc.scalar.activation(weighted[:, t, :], sig[t // 2][:, t % 2, first:last], ACT.Copy, scale=gain_scaled[:, t : t + 1])
 
         k1_picked = [placed("k1_picked%d" % h, [P, HALF], U32, 8192 - 512 + 2048 * h)[:] for h in range(2)]
         gather_keys(k1_picked, k1_list)
@@ -141,8 +153,8 @@ def tile_picked_scoregate_sigmoid_po_kernel(
         w_plane = placed("w_plane", [P, N], U8, 8192)
         w_codes = placed("w_codes", [P, 2 * N], U8, 8192 - 1024)
         deal_bytes(w_plane[:], w_bytes[:])
-        nc.vector.tensor_copy(w_codes[:].rearrange("p (t m b) -> p t m b", t=PACK, b=2),
-                              w_words[:].rearrange("p (m t b) -> p t m b", t=PACK, b=2))
+        nc.vector.tensor_copy(w_codes[:].bitcast(U16).rearrange("p (t m) -> p t m", t=PACK),
+                              w_words[:].bitcast(U16).rearrange("p (m t) -> p t m", t=PACK))
 
         z_codes = tile("z_codes", [P, S], U32)
         z_plane = tile("z_plane", [P, S], U8)
@@ -150,6 +162,7 @@ def tile_picked_scoregate_sigmoid_po_kernel(
         y_plane = tile("y_plane", [P, S], U8)
         out_rows = out_0.rearrange("(p t) j -> p t j", t=PACK)
         out_words = out_1[0].rearrange("p c r -> p (c r)").bitcast(I32)
+        y_first = tile("y_first", [P, 2, PACK, CH], F32)
         scores, zs, ys, yr = {}, {}, {}, {}
 
         def chunk(c):
@@ -162,11 +175,12 @@ def tile_picked_scoregate_sigmoid_po_kernel(
                 nc.tensor.matmul_mx(out=scores[c][:, t, :], lhsT=k1_codes[:, cols].bitcast(FP8X4), lhsT_scale=late_planes[:, cols],
                                     rhs=x_codes[c // 2][:, chunk(c % 2)].bitcast(FP8X4), rhs_scale=x_plane[:, chunk(c)], start=True, stop=True)
 
-        def form_z(c):
-            zs[c] = placed("z%d" % c, [P, CH, PACK], BF16, 16384 + 1024 * c)
-            nc.vector.tensor_tensor(zs[c][:].rearrange("p (c i) t -> p c t i", i=2),
-                                    scores[c][:].rearrange("p t (c i) -> p c t i", i=2),
-                                    gate[c // 2][:, :, chunk(c % 2)].rearrange("p t (c i) -> p c t i", i=2), ALU.mult)
+        def form_z(c, first=0, last=CH):
+            if first == 0:
+                zs[c] = placed("z%d" % c, [P, CH, PACK], BF16, 16384 + 1024 * c)
+            nc.vector.tensor_tensor(zs[c][:, first:last, :].rearrange("p (c i) t -> p c t i", i=2),
+                                    scores[c][:, :, first:last].rearrange("p t (c i) -> p c t i", i=2),
+                                    gate[c][:, :, first:last].rearrange("p t (c i) -> p c t i", i=2), ALU.mult)
 
         def quantize_z(c):
             nc.vector.quantize_mx(out=z_codes[:, chunk(c)].bitcast(FP8X4), scales=z_plane[:, chunk(c)],
@@ -178,37 +192,35 @@ def tile_picked_scoregate_sigmoid_po_kernel(
                 nc.tensor.matmul_mx(out=y_bank[:, t, :], lhsT=w_codes[:, 2 * t * P : 2 * (t + 1) * P].bitcast(FP4X4),
                                     lhsT_scale=w_plane[:, t * P : (t + 1) * P],
                                     rhs=z_codes[:, chunk(c)].bitcast(FP8X4), rhs_scale=z_plane[:, chunk(c)], start=True, stop=True)
-            ys[c] = tile("y%d" % c, [P, PACK, CH], F32)
-            nc.scalar.copy(ys[c][:], y_bank[:])
-            nc.sync.dma_start(out_rows[:, :, chunk(c)], ys[c][:])
+            ys[c] = y_first[:, c] if c < 2 else tile("y%d" % c, [P, PACK, CH], F32)[:]
+            nc.scalar.copy(ys[c], y_bank[:])
+            nc.sync.dma_start(out_rows[:, :, chunk(c)], ys[c])
             if c == NCH - 1:
                 yr[c] = tile("yr%d" % c, [P, CH, PACK], BF16)
                 nc.scalar.copy(yr[c][:], y_bank[:].rearrange("p t j -> p j t"))
 
-        def round_y(c):
-            yr[c] = placed("yr%d" % c, [P, CH, PACK], BF16, 16384 + 1024 * (NCH - 2 - c))
-            nc.vector.tensor_copy(yr[c][:].rearrange("p (c i) t -> p c t i", i=2), ys[c][:].rearrange("p t (c i) -> p c t i", i=2))
-
-        def quantize_y(c):
-            nc.vector.quantize_mx(out=y_codes[:, chunk(c)].bitcast(FP8X4), scales=y_plane[:, chunk(c)],
-                                  in_=yr[c][:].rearrange("p j t -> p (j t)"))
-            if c >= NCH - 2:
-                cols = chunk(c) if c == NCH - 1 else slice(0, (c + 1) * CH)
-                nc.sync.dma_start(out_words[:, cols], y_codes[:, cols].bitcast(I32))
+        def quantize_y(cols, rounded):
+            nc.vector.quantize_mx(out=y_codes[:, cols].bitcast(FP8X4), scales=y_plane[:, cols], in_=rounded)
 
         for c in range(NCH):
             score(c)
-        for c in range(NCH + 1):
+        form_z(0)
+        for c in range(1, NCH + 1):
             if c < NCH:
-                form_z(c)
-            if c >= 1:
-                quantize_z(c - 1)
-                project(c - 1)
-        for c in range(NCH + 1):
-            if c < NCH - 1:
-                round_y(c)
-            if c >= 1:
-                quantize_y(c - 1)
+                form_z(c, 0, CH // 2 if c == 1 else CH)
+            quantize_z(c - 1)
+            project(c - 1)
+            if c == 1:
+                form_z(c, CH // 2, CH)
+        yr_first = placed("yr_first", [P, 2, CH, PACK], BF16, 16384 + 1024)
+        nc.vector.tensor_copy(yr_first[:].rearrange("p h (c i) t -> p h c t i", i=2), y_first[:].rearrange("p h t (c i) -> p h c t i", i=2))
+        yr[2] = placed("yr2", [P, CH, PACK], BF16, 16384)
+        nc.vector.tensor_copy(yr[2][:].rearrange("p (c i) t -> p c t i", i=2), ys[2].rearrange("p t (c i) -> p c t i", i=2))
+        quantize_y(slice(0, HALF), yr_first[:].rearrange("p h j t -> p (h j t)"))
+        nc.sync.dma_start(out_words[:, 0:HALF], y_codes[:, 0:HALF].bitcast(I32))
+        for c in (2, 3):
+            quantize_y(chunk(c), yr[c][:].rearrange("p j t -> p (j t)"))
+        nc.sync.dma_start(out_words[:, HALF:S], y_codes[:, HALF:S].bitcast(I32))
         for q in range(4):
             queue = nc.scalar if q % 2 else nc.sync
             queue.dma_start(out_2[0, 4 * q : 4 * q + 4, :].bitcast(I32), y_plane[32 * q : 32 * q + 4, :].bitcast(I32))

@@ -49,24 +49,24 @@ def tile_picked_scoregate_sigmoid_po_kernel(
         x_byte_table = tile("x_byte_table", [P, T], U8)
         d_word_table = tile("d_word_table", [P, G], I32)
         x_word_table = tile("x_word_table", [P, T], I32)
-        gain = tile("gain", [P, PACK], F32)
+        gain = placed("gain", [P, 32], F32, 28672 - 64)[:, 0:PACK]
         gain_scaled = tile("gain_scaled", [P, PACK], F32)
         warm = tile("warm", [P, PACK], F32)
 
         nc.sync.dma_start(offs_list[:], offs)
         nc.vector.memset(d_byte_table[:].bitcast(I32), 0)
-        nc.scalar.dma_start(x_byte_table[0:32, :].bitcast(I32), x_scales[0].bitcast(I32).unsqueeze(1).to_broadcast([16, 2, T // 4]))
+        nc.sync.dma_start(x_byte_table[0:32, :].bitcast(I32), x_scales[0].bitcast(I32).unsqueeze(1).to_broadcast([16, 2, T // 4]))
         for first, last in ((32, 64), (64, P)):
             nc.vector.memset(x_byte_table[first:last, :].bitcast(I32), 0)
         nc.sync.dma_start(k2_list[:], k2)
         nc.sync.dma_start(k1_list[:], k1)
-        nc.sync.dma_start(gain[:], gn.rearrange("(p t) o -> p (t o)", t=PACK))
         nc.sync.dma_start(d_byte_table[0:P:8, :].bitcast(I32), d_scales[0].bitcast(I32))
         nc.sync.dma_start(d_word_table[:], d_words[0].rearrange("p c r -> p (c r)").bitcast(I32))
         nc.sync.dma_start(x_word_table[:], x_words[0].rearrange("p c r -> p (c r)").bitcast(I32))
+        nc.sync.dma_start(gain, gn.rearrange("(p t) o -> p (t o)", t=PACK))
         nc.gpsimd.memset(warm[:, 0:1], 0.0)
         nc.scalar.activation(warm[:, 1:2], warm[:, 0:1], ACT.Sigmoid)
-        nc.gpsimd.tensor_scalar_mul(gain_scaled[:], gain[:], SCORE_SCALE)
+        nc.scalar.activation(gain_scaled[:], gain, ACT.Copy, scale=SCORE_SCALE)
 
         def gather_keys(picked, offsets):
             for h in range(2):
@@ -89,11 +89,12 @@ def tile_picked_scoregate_sigmoid_po_kernel(
         x_plane = tile("x_plane", [P, S], U8)
         nc.vector.memset(x_plane[:].bitcast(I32), 0)
         k2_bytes = tile("k2_bytes", [P, H], U8)
-        x_bytes = placed("x_bytes", [P, S], U8, 28672 - HALF)
+        x_bytes = tile("x_bytes", [P, S], U8)
         nc.vector.tensor_copy(x_bytes[:], x_byte_table[:].indirect(offs_list[:]))
         nc.vector.tensor_copy(k2_bytes[:], d_byte_table[:].indirect(k2_list[:]))
         for q in range(4):
-            nc.sync.dma_start(x_plane[32 * q : 32 * q + 4, :].bitcast(I32), x_bytes[8 * q : 8 * q + 8 : 2, :].bitcast(I32))
+            queue = nc.scalar if q else nc.gpsimd
+            queue.dma_start(x_plane[32 * q : 32 * q + 4, :].bitcast(I32), x_bytes[8 * q : 8 * q + 8 : 2, :].bitcast(I32))
         k1_bytes = [tile("k1_bytes0", [P, HALF], U8), placed("k1_bytes1", [P, HALF], U8, 28672)]
 
         def gather_late_bytes(h):
@@ -217,10 +218,9 @@ def tile_picked_scoregate_sigmoid_po_kernel(
         yr[2] = placed("yr2", [P, CH, PACK], BF16, 16384)
         nc.vector.tensor_copy(yr[2][:].rearrange("p (c i) t -> p c t i", i=2), ys[2].rearrange("p t (c i) -> p c t i", i=2))
         quantize_y(slice(0, HALF), yr_first[:].rearrange("p h j t -> p (h j t)"))
-        nc.sync.dma_start(out_words[:, 0:HALF], y_codes[:, 0:HALF].bitcast(I32))
-        for c in (2, 3):
+        for c, cols in ((2, slice(0, 3 * CH)), (3, chunk(3))):
             quantize_y(chunk(c), yr[c][:].rearrange("p j t -> p (j t)"))
-        nc.sync.dma_start(out_words[:, HALF:S], y_codes[:, HALF:S].bitcast(I32))
+            nc.sync.dma_start(out_words[:, cols], y_codes[:, cols].bitcast(I32))
         for q in range(4):
             queue = nc.scalar if q % 2 else nc.sync
             queue.dma_start(out_2[0, 4 * q : 4 * q + 4, :].bitcast(I32), y_plane[32 * q : 32 * q + 4, :].bitcast(I32))

@@ -198,7 +198,7 @@ def tile_picked_scoregate_sigmoid_po_kernel(
             nc.sync.dma_start(out_rows[:, :, chunk(c)], ys[c])
             if c == NCH - 1:
                 yr[c] = tile("yr%d" % c, [P, CH, PACK], BF16)
-                nc.scalar.copy(yr[c][:], y_bank[:].rearrange("p t j -> p j t"))
+                nc.scalar.copy(yr[c][:].rearrange("p (c i) t -> p c t i", i=2), y_bank[:].rearrange("p t (c i) -> p c t i", i=2))
 
         def quantize_y(cols, rounded):
             nc.vector.quantize_mx(out=y_codes[:, cols].bitcast(FP8X4), scales=y_plane[:, cols], in_=rounded)

@@ -208,10 +208,10 @@ def tile_picked_scoregate_sigmoid_po_kernel(
         form_z(0)
         for c in range(1, NCH + 1):
             if c < NCH:
-                form_z(c, 0, CH // 2 if c == 1 else CH)
+                form_z(c, 0, CH // 2)
             quantize_z(c - 1)
             project(c - 1)
-            if c == 1:
+            if c < NCH:
                 form_z(c, CH // 2, CH)
         yr_first = placed("yr_first", [P, 2, CH, PACK], BF16, 16384 + 1024)
         nc.vector.tensor_copy(yr_first[:].rearrange("p h (c i) t -> p h c t i", i=2), y_first[:].rearrange("p h t (c i) -> p h c t i", i=2))

from contextlib import ExitStack

import concourse.mybir as mybir

K, T, S, N, G, H = 512, 2048, 512, 512, 2048, 512
FLOPS = 2 * K * H * S * 2 + 2 * H * N * S

F32 = mybir.dt.float32
BF16 = mybir.dt.bfloat16
I32 = mybir.dt.int32
U32 = mybir.dt.uint32
U16 = mybir.dt.uint16
U8 = mybir.dt.uint8
FP8X4 = mybir.dt.float8_e4m3fn_x4
FP4X4 = mybir.dt.float4_e2m1fn_x4
ACT = mybir.ActivationFunctionType
ALU = mybir.AluOpType

P = 128
PACK = 4
CH = 128
NCH = S // CH
SCORE_SCALE = 0.0625
HALF = H // 2


def tile_picked_scoregate_sigmoid_po_kernel(
    tc, x_words, x_scales, d_words, d_scales, gn, w1_words, w1_scales, offs, k1, k2, out_0, out_1, out_2
):
    nc = tc.nc
    with ExitStack() as ctx:
        sb = ctx.enter_context(tc.tile_pool(name="sb", bufs=1))
        reuse = ctx.enter_context(tc.tile_pool(name="reuse", bufs=1))
        psum = ctx.enter_context(tc.psum_pool(name="psum", bufs=1))

        def tile(name, shape, dtype):
            return sb.tile(shape, dtype, name=name, tag=name, align_bytes=64)

        def placed(name, shape, dtype, offset):
            return reuse.tile(shape, dtype, name=name, align_bytes=64, offset=offset)

        def bank(name, shape, number):
            return psum.tile(shape, F32, name=name, tag="bank%d" % number)

        k1_list = sb.tile([P, H // 16], U16, name="k1_list")
        offs_list = sb.tile([P, S // 16], U16, name="offs_list")
        k2_list = sb.tile([P, H // 16], U16, name="k2_list")
        d_byte_table = placed("d_byte_table", [P, G], U8, 8192)
        x_byte_table = tile("x_byte_table", [P, T], U8)
        d_word_table = tile("d_word_table", [P, G], I32)
        x_word_table = tile("x_word_table", [P, T], I32)
        gain = placed("gain", [P, 32], F32, 28672 - 64)[:, 0:PACK]
        gain_scaled = tile("gain_scaled", [P, PACK], F32)
        warm = tile("warm", [P, PACK], F32)

        nc.sync.dma_start(offs_list[:], offs)
        nc.vector.memset(d_byte_table[:].bitcast(I32), 0)
        nc.sync.dma_start(x_byte_table[0:32, :].bitcast(I32), x_scales[0].bitcast(I32).unsqueeze(1).to_broadcast([16, 2, T // 4]))
        for first, last in ((32, 64), (64, P)):
            nc.vector.memset(x_byte_table[first:last, :].bitcast(I32), 0)
        nc.sync.dma_start(k2_list[:], k2)
        nc.sync.dma_start(k1_list[:], k1)
        nc.sync.dma_start(d_byte_table[0:P:8, :].bitcast(I32), d_scales[0].bitcast(I32))
        nc.sync.dma_start(d_word_table[:], d_words[0].rearrange("p c r -> p (c r)").bitcast(I32))
        nc.sync.dma_start(x_word_table[:], x_words[0].rearrange("p c r -> p (c r)").bitcast(I32))
        nc.sync.dma_start(gain, gn.rearrange("(p t) o -> p (t o)", t=PACK))
        nc.gpsimd.memset(warm[:, 0:1], 0.0)
        nc.scalar.activation(warm[:, 1:2], warm[:, 0:1], ACT.Sigmoid)
        nc.scalar.activation(gain_scaled[:], gain, ACT.Copy, scale=SCORE_SCALE)

        def gather_keys(picked, offsets):
            for h in range(2):
                nc.vector.tensor_copy(picked[h], d_word_table[:].bitcast(U32).indirect(offsets[:, h * HALF // 16 : (h + 1) * HALF // 16]))

        def deal_keys(codes, picked):
            dst = codes[:].bitcast(I32).rearrange("p (t h m) -> p h m t", t=PACK, h=2)
            for h in range(2):
                nc.vector.tensor_copy(dst[:, h], picked[h].bitcast(I32).rearrange("p (m t) -> p m t", t=PACK))

        def deal_bytes(plane, source):
            nc.vector.tensor_copy(plane.rearrange("p (t m) -> p t m", t=PACK), source.rearrange("p (m t) -> p t m", t=PACK))

        def place_scale_rows(planes, queues):
            rows = planes[:].bitcast(I32)
            for r in range(1, PACK):
                queues[r - 1].dma_start(rows[r:P:32, :], rows[8 * r : P : 32, :])

        gate_planes = tile("gate_planes", [P, H], U8)
        x_plane = tile("x_plane", [P, S], U8)
        nc.vector.memset(x_plane[:].bitcast(I32), 0)
        k2_bytes = tile("k2_bytes", [P, H], U8)
        x_bytes = tile("x_bytes", [P, S], U8)
        nc.vector.tensor_copy(x_bytes[:], x_byte_table[:].indirect(offs_list[:]))
        nc.vector.tensor_copy(k2_bytes[:], d_byte_table[:].indirect(k2_list[:]))
        for q in range(4):
            queue = nc.scalar if q else nc.gpsimd
            queue.dma_start(x_plane[32 * q : 32 * q + 4, :].bitcast(I32), x_bytes[8 * q : 8 * q + 8 : 2, :].bitcast(I32))
        k1_bytes = [tile("k1_bytes0", [P, HALF], U8), placed("k1_bytes1", [P, HALF], U8, 28672)]

        def gather_late_bytes(h):
            nc.vector.tensor_copy(k1_bytes[h][:], d_byte_table[:].indirect(k1_list[:, h * HALF // 16 : (h + 1) * HALF // 16]))

        gather_late_bytes(0)
        deal_bytes(gate_planes[:, 0:H], k2_bytes[:])
        place_scale_rows(gate_planes, (nc.scalar, nc.scalar, nc.scalar))
        k2_picked = [placed("k2_picked%d" % h, [P, HALF], U32, 12288 + 2048 * h)[:] for h in range(2)]
        gather_keys(k2_picked, k2_list)
        k2_codes = tile("k2_codes", [P, H], U32)
        deal_keys(k2_codes, k2_picked)
        w_bytes = placed("w_bytes", [P, N], U8, 12288)
        w_words = placed("w_words", [P, 2 * N], U8, 12288 + N)
        nc.sync.dma_start(w_words[:].bitcast(I32), w1_words[0].bitcast(I32))
        w_rows = w1_scales[0].bitcast(I32)
        for q in range(4):
            nc.sync.dma_start(w_bytes[32 * q : 32 * q + 32, :].bitcast(I32),
                              w_rows[4 * q : 4 * q + 4, :].unsqueeze(0).to_broadcast([8, 4, N // 4]))
        late_planes = placed("late_planes", [P, H], U8, 28672 - H)
        x_codes = [tile("x_codes0", [P, HALF], U32)]

        def gather_queries(h):
            nc.vector.tensor_copy(x_codes[h][:],
                                  x_word_table[:].bitcast(U32).indirect(offs_list[:, h * HALF // 16 : (h + 1) * HALF // 16]))

        gather_queries(0)
        gather_late_bytes(1)
        late_slots = late_planes[:].rearrange("p (t h m) -> p h t m", t=PACK, h=2)
        for h in range(2):
            nc.vector.tensor_copy(late_slots[:, h], k1_bytes[h][:].rearrange("p (m t) -> p t m", t=PACK))
        place_scale_rows(late_planes, (nc.sync, nc.sync, nc.sync))
        x_codes.append(placed("x_codes1", [P, HALF], U32, 8192 + 512))
        gather_queries(1)

        first_gate = tile("first_gate", [P, PACK, HALF], F32)
        gate = [first_gate[:, :, 0:CH], first_gate[:, :, CH:HALF]] + [tile("gate%d" % c, [P, PACK, CH], F32)[:] for c in (2, 3)]
        for h in range(2):
            sig = [tile("sig%d%d" % (h, u), [P, 2, HALF], F32) for u in range(2)]
            js = slice(h * HALF, (h + 1) * HALF)
            for u in range(2):
                b_bank = bank("b_bank", [P, 2, HALF], PACK + 2 * h + u)
                for v in range(2):
                    cols = slice((2 * u + v) * P, (2 * u + v + 1) * P)
                    nc.tensor.matmul_mx(out=b_bank[:, v, :], lhsT=k2_codes[:, cols].bitcast(FP8X4), lhsT_scale=gate_planes[:, cols],
                                        rhs=x_codes[h][:].bitcast(FP8X4), rhs_scale=x_plane[:, js], start=True, stop=True)
                nc.scalar.activation(sig[u][:], b_bank[:], ACT.Sigmoid, scale=SCORE_SCALE)
            pieces = [(first_gate[:], 0, HALF)] if h == 0 else [(gate[2], 0, CH), (gate[3], CH, HALF)]
            for weighted, first, last in pieces:
                for t in range(PACK):
                    nc.scalar.activation(weighted[:, t, :], sig[t // 2][:, t % 2, first:last], ACT.Copy, scale=gain_scaled[:, t : t + 1])

        k1_picked = [placed("k1_picked%d" % h, [P, HALF], U32, 8192 - 512 + 2048 * h)[:] for h in range(2)]
        gather_keys(k1_picked, k1_list)
        k1_codes = tile("k1_codes", [P, H], U32)
        deal_keys(k1_codes, k1_picked)
        w_plane = placed("w_plane", [P, N], U8, 8192)
        w_codes = placed("w_codes", [P, 2 * N], U8, 8192 - 1024)
        deal_bytes(w_plane[:], w_bytes[:])
        nc.vector.tensor_copy(w_codes[:].bitcast(U16).rearrange("p (t m) -> p t m", t=PACK),
                              w_words[:].bitcast(U16).rearrange("p (m t) -> p t m", t=PACK))

        z_codes = tile("z_codes", [P, S], U32)
        z_plane = tile("z_plane", [P, S], U8)
        y_codes = tile("y_codes", [P, S], U32)
        y_plane = tile("y_plane", [P, S], U8)
        out_rows = out_0.rearrange("(p t) j -> p t j", t=PACK)
        out_words = out_1[0].rearrange("p c r -> p (c r)").bitcast(I32)
        y_first = tile("y_first", [P, 2, PACK, CH], F32)
        scores, zs, ys, yr = {}, {}, {}, {}

        def chunk(c):
            return slice(c * CH, (c + 1) * CH)

        def score(c):
            scores[c] = bank("a_bank", [P, PACK, CH], c)
            for t in range(PACK):
                cols = slice(t * P, (t + 1) * P)
                nc.tensor.matmul_mx(out=scores[c][:, t, :], lhsT=k1_codes[:, cols].bitcast(FP8X4), lhsT_scale=late_planes[:, cols],
                                    rhs=x_codes[c // 2][:, chunk(c % 2)].bitcast(FP8X4), rhs_scale=x_plane[:, chunk(c)], start=True, stop=True)

        def form_z(c, first=0, last=CH):
            if first == 0:
                zs[c] = placed("z%d" % c, [P, CH, PACK], BF16, 16384 + 1024 * c)
            nc.vector.tensor_tensor(zs[c][:, first:last, :].rearrange("p (c i) t -> p c t i", i=2),
                                    scores[c][:, :, first:last].rearrange("p t (c i) -> p c t i", i=2),
                                    gate[c][:, :, first:last].rearrange("p t (c i) -> p c t i", i=2), ALU.mult)

        def quantize_z(c):
            nc.vector.quantize_mx(out=z_codes[:, chunk(c)].bitcast(FP8X4), scales=z_plane[:, chunk(c)],
                                  in_=zs[c][:].rearrange("p j t -> p (j t)"))

        def project(c):
            y_bank = bank("y_bank", [P, PACK, CH], PACK + c)
            for t in range(PACK):
                nc.tensor.matmul_mx(out=y_bank[:, t, :], lhsT=w_codes[:, 2 * t * P : 2 * (t + 1) * P].bitcast(FP4X4),
                                    lhsT_scale=w_plane[:, t * P : (t + 1) * P],
                                    rhs=z_codes[:, chunk(c)].bitcast(FP8X4), rhs_scale=z_plane[:, chunk(c)], start=True, stop=True)
            ys[c] = y_first[:, c] if c < 2 else tile("y%d" % c, [P, PACK, CH], F32)[:]
            nc.scalar.copy(ys[c], y_bank[:])
            nc.sync.dma_start(out_rows[:, :, chunk(c)], ys[c])
            if c == NCH - 1:
                yr[c] = tile("yr%d" % c, [P, CH, PACK], BF16)
                nc.scalar.copy(yr[c][:].rearrange("p (c i) t -> p c t i", i=2), y_bank[:].rearrange("p t (c i) -> p c t i", i=2))

        def quantize_y(cols, rounded):
            nc.vector.quantize_mx(out=y_codes[:, cols].bitcast(FP8X4), scales=y_plane[:, cols], in_=rounded)

        for c in range(NCH):
            score(c)
        form_z(0)
        for c in range(1, NCH + 1):
            if c < NCH:
                form_z(c, 0, CH // 2)
            quantize_z(c - 1)
            project(c - 1)
            if c < NCH:
                form_z(c, CH // 2, CH)
        yr_first = placed("yr_first", [P, 2, CH, PACK], BF16, 16384 + 1024)
        nc.vector.tensor_copy(yr_first[:].rearrange("p h (c i) t -> p h c t i", i=2), y_first[:].rearrange("p h t (c i) -> p h c t i", i=2))
        yr[2] = placed("yr2", [P, CH, PACK], BF16, 16384)
        nc.vector.tensor_copy(yr[2][:].rearrange("p (c i) t -> p c t i", i=2), ys[2].rearrange("p t (c i) -> p c t i", i=2))
        quantize_y(slice(0, HALF), yr_first[:].rearrange("p h j t -> p (h j t)"))
        for c, cols in ((2, slice(0, 3 * CH)), (3, chunk(3))):
            quantize_y(chunk(c), yr[c][:].rearrange("p j t -> p (j t)"))
            nc.sync.dma_start(out_words[:, cols], y_codes[:, cols].bitcast(I32))
        for q in range(4):
            queue = nc.scalar if q % 2 else nc.sync
            queue.dma_start(out_2[0, 4 * q : 4 * q + 4, :].bitcast(I32), y_plane[32 * q : 32 * q + 4, :].bitcast(I32))
